import numpy as np
import ml_dtypes


def mxq(x, axis, fmt="e4m3"):
    dtype, down = {"e4m3": (ml_dtypes.float8_e4m3fn, 7), "e5m2": (ml_dtypes.float8_e5m2, 14)}[fmt]
    v = np.moveaxis(np.asarray(x, np.float32).astype(ml_dtypes.bfloat16).astype(np.float64), axis, -1)
    blocks = v.reshape(v.shape[:-1] + (-1, 32))
    amax = np.abs(blocks).max(-1, keepdims=True)
    byte = np.maximum(np.where(amax > 0, np.frexp(amax)[1] - 1 + 127, 0) - down, 1)
    scale = np.exp2(byte - 127.0)
    codes = (blocks / scale).astype(np.float32).astype(dtype).astype(np.float64)
    return np.moveaxis((codes * scale).reshape(v.shape), -1, axis)


WIDE = False


def mx_kscale(k):
    if not WIDE:
        return np.ones(k)
    levels = np.array([10, -10, 5, -5, 0])
    if k % 512:
        return np.exp2(np.random.permutation(np.resize(levels, k // 32))).repeat(32)
    a = np.empty((k // 512, 16))
    for p in range(k // 512):
        a[p, :8] = np.random.permutation(np.resize(levels, 8))
        for g in range(8):
            far = levels[np.abs(levels - a[p, g]) >= 10]
            a[p, g + 8] = far[np.random.randint(len(far))]
    return np.exp2(a.ravel()).repeat(32)


def f64(x):
    return np.asarray(x).astype(np.float64)


def striped(idx):
    return np.tile(idx.reshape(-1, 16).T, (8, 1)).astype(np.uint16)


def unstriped(offs):
    return offs[:16].T.reshape(-1).astype(np.int64)


def pack_weight(w):
    k, n = w.shape
    w = f64(np.asarray(w, np.float32).astype(ml_dtypes.bfloat16)).reshape(k // 32, 32, n)
    amax = np.abs(w).max(1)
    byte = np.clip(np.where(amax > 0, np.frexp(amax)[1] - 1 + 127 - 7, 1), 1, 254)
    scaled = (w * np.exp2(127.0 - byte)[:, None, :]).reshape(k, n).astype(np.float32)
    words = np.ascontiguousarray(scaled.reshape(k // 512, 128, 4, n).transpose(0, 1, 3, 2)).astype(ml_dtypes.float8_e4m3fn).view(np.uint8)
    return words, np.ascontiguousarray(byte.astype(np.uint8).reshape(k // 512, 16, n))


def unpack_weight(words, scales):
    g, p, n, _ = words.shape
    vals = np.ascontiguousarray(words).view(ml_dtypes.float8_e4m3fn).astype(np.float64) * np.repeat(np.exp2(scales.astype(np.float64) - 127.0), 8, axis=1)[..., None]
    return vals.transpose(0, 1, 3, 2).reshape(g * 512, n)


def sigmoid(v):
    return 1.0 / (1.0 + np.exp(-np.maximum(v, -700.0)))


K, T, S, N, D = 1024, 1024, 512, 128, 2
P = 2 ** 7


def setup_inputs():
    n = np.random.standard_normal
    s = mx_kscale(K)[:, None]
    packed_xT = pack_weight(n((K, T)) * s)
    return {
        "x_words": packed_xT[0],
        "x_scales": packed_xT[1],
        "w1": (n((K, N)) / np.sqrt(K) / s).astype(np.float32),
        "gate": (np.tile(np.random.uniform(0.2, 0.5, (D, 1, S)), (1, P, 1))).astype(np.float32),
        "rate": (np.random.uniform(0.1, 0.8, (N, 1))).astype(np.float32),
        "offs": striped(np.random.permutation(T)[:S]),
        "pos1": striped(np.random.permutation(S)[:S]),
        "pos2": striped(np.random.permutation(S)[:S]),
    }


def reference(x_words, x_scales, w1, gate, rate, offs, pos1, pos2):
    xq = unpack_weight(x_words, x_scales)[:, unstriped(offs)]
    y = sigmoid(mxq(f64(w1), 0, "e4m3").T @ xq)
    dd = y[:, unstriped(pos1)] * f64(gate)[0, :1] + y[:, unstriped(pos2)] * f64(gate)[1, :1] - y
    rr = y * y - ((y * y) * y)
    return y + 0.5 * dd + f64(rate) * rr

@@ -1,0 +1,126 @@
+from contextlib import ExitStack
+
+import concourse.mybir as mybir
+
+K, T, S, M = 1024, 1024, 512, 128
+FLOPS = 2 * K * M * S
+
+F32 = mybir.dt.float32
+BF16 = mybir.dt.bfloat16
+I32 = mybir.dt.int32
+U32 = mybir.dt.uint32
+U16 = mybir.dt.uint16
+U8 = mybir.dt.uint8
+FP8X4 = mybir.dt.float8_e4m3fn_x4
+ACT = mybir.ActivationFunctionType
+ALU = mybir.AluOpType
+
+P = 128
+PACK = 4
+PASSES = 2
+LANE = 16
+CHUNKS = ((0, 256), (256, 384), (384, 512))
+HALVES = ((0, 256), (256, 512))
+
+
+def tile_picked_ygread_zeld_p_kernel(tc, x_words, x_scales, w1, gate, rate, offs, pos1, pos2, out):
+    nc = tc.nc
+    with ExitStack() as ctx:
+        keep = ctx.enter_context(tc.tile_pool(name="keep", bufs=1))
+        psum = ctx.enter_context(tc.psum_pool(name="psum", bufs=1))
+
+        offs_sb = keep.tile([P, S // LANE], U16, name="offs_sb")
+        pos_sb = [keep.tile([P, S // LANE], U16, name=f"pos_sb{d}") for d in range(2)]
+        words = [keep.tile([P, T], U32, name=f"words{g}", align_bytes=64) for g in range(PASSES)]
+        scales = keep.tile([P, T], U8, name="scales", tag="scales", align_bytes=64)
+        w_raw = [keep.tile([P, PACK, M], F32, name=f"w_raw{g}") for g in range(PASSES)]
+        gate_sb = keep.tile([P, 2, S], F32, name="gate_sb")
+        rate_sb = keep.tile([P, 1], F32, name="rate_sb")
+
+        nc.vector.memset(scales[:].bitcast(I32), 0)
+        nc.sync.dma_start(offs_sb[:], offs)
+        for q in range(4):
+            nc.scalar.dma_start(
+                scales[32 * q : 32 * q + 8, :].bitcast(I32),
+                x_scales[:, 4 * q : 4 * q + 4, :].bitcast(I32),
+            )
+        for g in range(PASSES):
+            nc.sync.dma_start(w_raw[g][:], w1[512 * g : 512 * (g + 1), :].rearrange("(p j) m -> p j m", j=PACK))
+        for g in range(PASSES):
+            nc.sync.dma_start(words[g][:].bitcast(I32), x_words[g].rearrange("p c r -> p (c r)").bitcast(I32))
+        nc.sync.dma_start(rate_sb[:], rate)
+        nc.sync.dma_start(pos_sb[0][:], pos1)
+        nc.sync.dma_start(pos_sb[1][:], pos2)
+        nc.sync.dma_start(gate_sb[:], gate.rearrange("d p j -> p d j"))
+
+        w_bf = keep.tile([P, PASSES * M * PACK], BF16, name="w_bf", align_bytes=64)
+        for g in range(PASSES):
+            nc.scalar.copy(
+                w_bf[:, g * M * PACK : (g + 1) * M * PACK].rearrange("p (m j) -> p m j", j=PACK),
+                w_raw[g][:].rearrange("p j m -> p m j"),
+            )
+
+        picked = [keep.tile([P, S], U32, name=f"picked{g}", align_bytes=64) for g in range(PASSES)]
+        picked_scales = keep.tile([P, S], U8, name="picked_scales", align_bytes=64)
+        nc.vector.tensor_copy(picked_scales[:], scales[:].indirect(offs_sb[:]))
+
+        w_codes = keep.tile([P, PASSES * M], U32, name="w_codes", tag="scales", align_bytes=64)
+        w_scales = keep.tile([P, PASSES * M], U8, name="w_scales", align_bytes=64)
+        nc.vector.quantize_mx(out=w_codes[:].bitcast(FP8X4), scales=w_scales[:], in_=w_bf[:])
+        nc.vector.tensor_copy(picked[0][:], words[0][:].indirect(offs_sb[:]))
+
+        y = keep.tile([P, S], F32, name="y")
+        acc = [psum.tile([P, b - a], F32, name=f"acc{a}") for a, b in CHUNKS]
+
+        def product(c, g):
+            a, b = CHUNKS[c]
+            nc.tensor.matmul_mx(
+                out=acc[c][:],
+                lhsT=w_codes[:, g * M : (g + 1) * M].bitcast(FP8X4),
+                lhsT_scale=w_scales[:, g * M : (g + 1) * M],
+                rhs=picked[g][:, a:b].bitcast(FP8X4),
+                rhs_scale=picked_scales[4 * g : P, a:b],
+                start=(g == 0),
+                stop=(g == PASSES - 1),
+            )
+
+        for c in range(len(CHUNKS)):
+            product(c, 0)
+        for c, (a, b) in enumerate(CHUNKS):
+            nc.vector.tensor_copy(picked[1][:, a:b], words[1][:].indirect(offs_sb[:, a // LANE : b // LANE]))
+            product(c, 1)
+            nc.scalar.activation(y[:, a:b], acc[c][:], ACT.Sigmoid)
+
+        coef = keep.tile([P, 2], F32, name="coef")
+        nc.scalar.activation(coef[:, 0:1], rate_sb[:], ACT.Copy, scale=-1.0)
+        nc.scalar.activation(coef[:, 1:2], rate_sb[:], ACT.Copy, scale=0.25, bias=0.5)
+
+        sq = keep.tile([P, S], F32, name="sq")
+        own = keep.tile([P, S], F32, name="own")
+        nc.scalar.activation(sq[:], y[:], ACT.Square, bias=-0.5)
+        nc.scalar.activation(own[:], sq[:], ACT.Identity, scale=coef[:, 0:1], bias=coef[:, 1:2])
+
+        cut = 384
+        rest = S - cut
+        pulled = [keep.tile([P, cut], F32, name=f"pulled{d}") for d in range(2)]
+        base = keep.tile([P, S], F32, name="base")
+        part = keep.tile([P, S], F32, name="part")
+        res = keep.tile([P, S], F32, name="res")
+
+        def pull(dst, d, a, b):
+            nc.vector.tensor_tensor(dst, y[:].indirect(pos_sb[d][:, a // LANE : b // LANE]), gate_sb[:, d, a:b], ALU.mult)
+
+        def half_add(dst, pulled_part, other):
+            nc.vector.scalar_tensor_tensor(dst, pulled_part, 0.5, other, ALU.mult, ALU.add)
+
+        pull(pulled[0][:], 0, 0, cut)
+        pull(pulled[1][:], 1, 0, cut)
+        nc.vector.tensor_tensor(base[:], y[:], own[:], ALU.mult)
+        half_add(part[:, :cut], pulled[0][:], base[:, :cut])
+        pull(own[:, :rest], 0, cut, S)
+        half_add(res[:, :cut], pulled[1][:], part[:, :cut])
+        nc.sync.dma_start(out[:, :cut], res[:, :cut])
+        pull(pulled[0][:, :rest], 1, cut, S)
+        half_add(part[:, cut:], own[:, :rest], base[:, cut:])
+        half_add(res[:, cut:], pulled[0][:, :rest], part[:, cut:])
+        nc.scalar.dma_start(out[:, cut:], res[:, cut:])

@@ -32,26 +32,32 @@ def tile_picked_ygread_zeld_p_kernel(tc, x_words, x_scales, w1, gate, rate, offs
         offs_sb = keep.tile([P, S // LANE], U16, name="offs_sb")
         pos_sb = [keep.tile([P, S // LANE], U16, name=f"pos_sb{d}") for d in range(2)]
         words = [keep.tile([P, T], U32, name=f"words{g}", align_bytes=64) for g in range(PASSES)]
-        scales = keep.tile([P, T], U8, name="scales", tag="scales", align_bytes=64)
+        scales = keep.tile([P, T], U8, name="scales", align_bytes=64)
         w_raw = [keep.tile([P, PACK, M], F32, name=f"w_raw{g}") for g in range(PASSES)]
         gate_sb = keep.tile([P, 2, S], F32, name="gate_sb")
         rate_sb = keep.tile([P, 1], F32, name="rate_sb")
 
         nc.vector.memset(scales[:].bitcast(I32), 0)
+        def load_words(g):
+            nc.sync.dma_start(words[g][:].bitcast(I32), x_words[g].rearrange("p c r -> p (c r)").bitcast(I32))
+
+        def load_weights(g):
+            nc.sync.dma_start(w_raw[g][:], w1[512 * g : 512 * (g + 1), :].rearrange("(p j) m -> p j m", j=PACK))
+
         nc.sync.dma_start(offs_sb[:], offs)
+        load_words(0)
+        load_weights(0)
         for q in range(4):
-            nc.scalar.dma_start(
+            nc.sync.dma_start(
                 scales[32 * q : 32 * q + 8, :].bitcast(I32),
                 x_scales[:, 4 * q : 4 * q + 4, :].bitcast(I32),
             )
-        for g in range(PASSES):
-            nc.sync.dma_start(w_raw[g][:], w1[512 * g : 512 * (g + 1), :].rearrange("(p j) m -> p j m", j=PACK))
-        for g in range(PASSES):
-            nc.sync.dma_start(words[g][:].bitcast(I32), x_words[g].rearrange("p c r -> p (c r)").bitcast(I32))
-        nc.sync.dma_start(rate_sb[:], rate)
+        load_weights(1)
+        load_words(1)
+        nc.sync.dma_start(gate_sb[:], gate.rearrange("d p j -> p d j"))
         nc.sync.dma_start(pos_sb[0][:], pos1)
         nc.sync.dma_start(pos_sb[1][:], pos2)
-        nc.sync.dma_start(gate_sb[:], gate.rearrange("d p j -> p d j"))
+        nc.gpsimd.dma_start(rate_sb[:], rate)
 
         w_bf = keep.tile([P, PASSES * M * PACK], BF16, name="w_bf", align_bytes=64)
         for g in range(PASSES):
@@ -62,12 +68,17 @@ def tile_picked_ygread_zeld_p_kernel(tc, x_words, x_scales, w1, gate, rate, offs
 
         picked = [keep.tile([P, S], U32, name=f"picked{g}", align_bytes=64) for g in range(PASSES)]
         picked_scales = keep.tile([P, S], U8, name="picked_scales", align_bytes=64)
+        nc.vector.tensor_copy(picked[0][:], words[0][:].indirect(offs_sb[:]))
         nc.vector.tensor_copy(picked_scales[:], scales[:].indirect(offs_sb[:]))
 
-        w_codes = keep.tile([P, PASSES * M], U32, name="w_codes", tag="scales", align_bytes=64)
+        w_codes = keep.tile([P, PASSES * M], U32, name="w_codes", align_bytes=64)
         w_scales = keep.tile([P, PASSES * M], U8, name="w_scales", align_bytes=64)
-        nc.vector.quantize_mx(out=w_codes[:].bitcast(FP8X4), scales=w_scales[:], in_=w_bf[:])
-        nc.vector.tensor_copy(picked[0][:], words[0][:].indirect(offs_sb[:]))
+        for g in range(PASSES):
+            nc.vector.quantize_mx(
+                out=w_codes[:, g * M : (g + 1) * M].bitcast(FP8X4),
+                scales=w_scales[:, g * M : (g + 1) * M],
+                in_=w_bf[:, g * M * PACK : (g + 1) * M * PACK],
+            )
 
         y = keep.tile([P, S], F32, name="y")
         acc = [psum.tile([P, b - a], F32, name=f"acc{a}") for a, b in CHUNKS]

@@ -41,32 +41,29 @@ def tile_picked_ygread_zeld_p_kernel(tc, x_words, x_scales, w1, gate, rate, offs
         def load_words(g):
             nc.sync.dma_start(words[g][:].bitcast(I32), x_words[g].rearrange("p c r -> p (c r)").bitcast(I32))
 
-        def load_weights(g):
-            nc.sync.dma_start(w_raw[g][:], w1[512 * g : 512 * (g + 1), :].rearrange("(p j) m -> p j m", j=PACK))
-
         nc.sync.dma_start(offs_sb[:], offs)
         load_words(0)
-        load_weights(0)
         for q in range(4):
             nc.sync.dma_start(
                 scales[32 * q : 32 * q + 8, :].bitcast(I32),
                 x_scales[:, 4 * q : 4 * q + 4, :].bitcast(I32),
             )
-        load_weights(1)
+        for g in range(PASSES):
+            nc.sync.dma_start(w_raw[g][:], w1[512 * g : 512 * (g + 1), :].rearrange("(p j) m -> p j m", j=PACK))
         load_words(1)
         nc.sync.dma_start(gate_sb[:], gate.rearrange("d p j -> p d j"))
         nc.sync.dma_start(pos_sb[0][:], pos1)
         nc.sync.dma_start(pos_sb[1][:], pos2)
-        nc.gpsimd.dma_start(rate_sb[:], rate)
+        nc.sync.dma_start(rate_sb[:], rate)
 
-        w_bf = keep.tile([P, PASSES * M * PACK], BF16, name="w_bf", align_bytes=64)
+        w_bf = keep.tile([P, PASSES * M * PACK], BF16, name="w_bf", tag="w_bf", align_bytes=64)
         for g in range(PASSES):
             nc.scalar.copy(
                 w_bf[:, g * M * PACK : (g + 1) * M * PACK].rearrange("p (m j) -> p m j", j=PACK),
                 w_raw[g][:].rearrange("p j m -> p m j"),
             )
 
-        picked = [keep.tile([P, S], U32, name=f"picked{g}", align_bytes=64) for g in range(PASSES)]
+        picked = [keep.tile([P, S], U32, name="picked0", align_bytes=64)]
         picked_scales = keep.tile([P, S], U8, name="picked_scales", align_bytes=64)
         nc.vector.tensor_copy(picked[0][:], words[0][:].indirect(offs_sb[:]))
         nc.vector.tensor_copy(picked_scales[:], scales[:].indirect(offs_sb[:]))
@@ -80,6 +77,7 @@ def tile_picked_ygread_zeld_p_kernel(tc, x_words, x_scales, w1, gate, rate, offs
                 in_=w_bf[:, g * M * PACK : (g + 1) * M * PACK],
             )
 
+        picked.append(keep.tile([P, S], U32, name="picked1", tag="w_bf", align_bytes=64))
         y = keep.tile([P, S], F32, name="y")
         acc = [psum.tile([P, b - a], F32, name=f"acc{a}") for a, b in CHUNKS]
 

@@ -33,7 +33,7 @@ def tile_picked_ygread_zeld_p_kernel(tc, x_words, x_scales, w1, gate, rate, offs
         pos_sb = [keep.tile([P, S // LANE], U16, name=f"pos_sb{d}") for d in range(2)]
         words = [keep.tile([P, T], U32, name=f"words{g}", align_bytes=64) for g in range(PASSES)]
         scales = keep.tile([P, T], U8, name="scales", align_bytes=64)
-        w_raw = [keep.tile([P, PACK, M], F32, name=f"w_raw{g}") for g in range(PASSES)]
+        w_raw = [keep.tile([P, PACK, M], F32, name=f"w_raw{g}", tag=f"w_raw{g}", align_bytes=64) for g in range(PASSES)]
         gate_sb = keep.tile([P, 2, S], F32, name="gate_sb")
         rate_sb = keep.tile([P, 1], F32, name="rate_sb")
 
@@ -41,22 +41,25 @@ def tile_picked_ygread_zeld_p_kernel(tc, x_words, x_scales, w1, gate, rate, offs
         def load_words(g):
             nc.sync.dma_start(words[g][:].bitcast(I32), x_words[g].rearrange("p c r -> p (c r)").bitcast(I32))
 
+        def load_weights(g):
+            nc.sync.dma_start(w_raw[g][:], w1[512 * g : 512 * (g + 1), :].rearrange("(p j) m -> p j m", j=PACK))
+
         nc.sync.dma_start(offs_sb[:], offs)
         load_words(0)
+        load_weights(0)
         for q in range(4):
             nc.sync.dma_start(
                 scales[32 * q : 32 * q + 8, :].bitcast(I32),
                 x_scales[:, 4 * q : 4 * q + 4, :].bitcast(I32),
             )
-        for g in range(PASSES):
-            nc.sync.dma_start(w_raw[g][:], w1[512 * g : 512 * (g + 1), :].rearrange("(p j) m -> p j m", j=PACK))
+        load_weights(1)
         load_words(1)
         nc.sync.dma_start(gate_sb[:], gate.rearrange("d p j -> p d j"))
         nc.sync.dma_start(pos_sb[0][:], pos1)
         nc.sync.dma_start(pos_sb[1][:], pos2)
         nc.sync.dma_start(rate_sb[:], rate)
 
-        w_bf = keep.tile([P, PASSES * M * PACK], BF16, name="w_bf", tag="w_bf", align_bytes=64)
+        w_bf = keep.tile([P, PASSES * M * PACK], BF16, name="w_bf", align_bytes=64)
         for g in range(PASSES):
             nc.scalar.copy(
                 w_bf[:, g * M * PACK : (g + 1) * M * PACK].rearrange("p (m j) -> p m j", j=PACK),
@@ -77,7 +80,7 @@ def tile_picked_ygread_zeld_p_kernel(tc, x_words, x_scales, w1, gate, rate, offs
                 in_=w_bf[:, g * M * PACK : (g + 1) * M * PACK],
             )
 
-        picked.append(keep.tile([P, S], U32, name="picked1", tag="w_bf", align_bytes=64))
+        picked.append(keep.tile([P, S], U32, name="picked1", tag="w_raw1", align_bytes=64))
         y = keep.tile([P, S], F32, name="y")
         acc = [psum.tile([P, b - a], F32, name=f"acc{a}") for a, b in CHUNKS]
 
@@ -125,11 +128,11 @@ def tile_picked_ygread_zeld_p_kernel(tc, x_words, x_scales, w1, gate, rate, offs
         pull(pulled[0][:], 0, 0, cut)
         pull(pulled[1][:], 1, 0, cut)
         nc.vector.tensor_tensor(base[:], y[:], own[:], ALU.mult)
+        pull(sq[:, :rest], 0, cut, S)
         half_add(part[:, :cut], pulled[0][:], base[:, :cut])
-        pull(own[:, :rest], 0, cut, S)
+        half_add(part[:, cut:], sq[:, :rest], base[:, cut:])
         half_add(res[:, :cut], pulled[1][:], part[:, :cut])
         nc.sync.dma_start(out[:, :cut], res[:, :cut])
         pull(pulled[0][:, :rest], 1, cut, S)
-        half_add(part[:, cut:], own[:, :rest], base[:, cut:])
         half_add(res[:, cut:], pulled[0][:, :rest], part[:, cut:])
         nc.scalar.dma_start(out[:, cut:], res[:, cut:])

@@ -34,10 +34,14 @@ def tile_picked_ygread_zeld_p_kernel(tc, x_words, x_scales, w1, gate, rate, offs
         words = [keep.tile([P, T], U32, name=f"words{g}", align_bytes=64) for g in range(PASSES)]
         scales = keep.tile([P, T], U8, name="scales", align_bytes=64)
         w_raw = [keep.tile([P, PACK, M], F32, name=f"w_raw{g}", tag=f"w_raw{g}", align_bytes=64) for g in range(PASSES)]
-        gate_sb = keep.tile([P, 2, S], F32, name="gate_sb")
+        gate_sb = [keep.tile([P, S], F32, name=f"gate_sb{d}") for d in range(2)]
         rate_sb = keep.tile([P, 1], F32, name="rate_sb")
 
         nc.vector.memset(scales[:].bitcast(I32), 0)
+        warm = keep.tile([P, 2], F32, name="warm")
+        nc.vector.memset(warm[:, 0:1], 0.0)
+        nc.scalar.activation(warm[:, 1:2], warm[:, 0:1], ACT.Sigmoid)
+
         def load_words(g):
             nc.sync.dma_start(words[g][:].bitcast(I32), x_words[g].rearrange("p c r -> p (c r)").bitcast(I32))
 
@@ -46,18 +50,19 @@ def tile_picked_ygread_zeld_p_kernel(tc, x_words, x_scales, w1, gate, rate, offs
 
         nc.sync.dma_start(offs_sb[:], offs)
         load_words(0)
-        load_weights(0)
         for q in range(4):
             nc.sync.dma_start(
                 scales[32 * q : 32 * q + 8, :].bitcast(I32),
                 x_scales[:, 4 * q : 4 * q + 4, :].bitcast(I32),
             )
+        load_weights(0)
         load_weights(1)
         load_words(1)
-        nc.sync.dma_start(gate_sb[:], gate.rearrange("d p j -> p d j"))
         nc.sync.dma_start(pos_sb[0][:], pos1)
-        nc.sync.dma_start(pos_sb[1][:], pos2)
+        nc.sync.dma_start(gate_sb[0][:], gate[0])
         nc.sync.dma_start(rate_sb[:], rate)
+        nc.sync.dma_start(pos_sb[1][:], pos2)
+        nc.sync.dma_start(gate_sb[1][:], gate[1])
 
         w_bf = keep.tile([P, PASSES * M * PACK], BF16, name="w_bf", align_bytes=64)
         for g in range(PASSES):
@@ -109,30 +114,25 @@ def tile_picked_ygread_zeld_p_kernel(tc, x_words, x_scales, w1, gate, rate, offs
 
         sq = keep.tile([P, S], F32, name="sq")
         own = keep.tile([P, S], F32, name="own")
-        nc.scalar.activation(sq[:], y[:], ACT.Square, bias=-0.5)
-        nc.scalar.activation(own[:], sq[:], ACT.Identity, scale=coef[:, 0:1], bias=coef[:, 1:2])
+        for a, b in HALVES:
+            nc.scalar.activation(sq[:, a:b], y[:, a:b], ACT.Square, bias=-0.5)
+        for a, b in HALVES:
+            nc.scalar.activation(own[:, a:b], sq[:, a:b], ACT.Identity, scale=coef[:, 0:1], bias=coef[:, 1:2])
 
-        cut = 384
-        rest = S - cut
-        pulled = [keep.tile([P, cut], F32, name=f"pulled{d}") for d in range(2)]
+        pulled = [keep.tile([P, S], F32, name=f"pulled{d}") for d in range(2)]
+        both = keep.tile([P, S], F32, name="both")
         base = keep.tile([P, S], F32, name="base")
-        part = keep.tile([P, S], F32, name="part")
         res = keep.tile([P, S], F32, name="res")
 
-        def pull(dst, d, a, b):
-            nc.vector.tensor_tensor(dst, y[:].indirect(pos_sb[d][:, a // LANE : b // LANE]), gate_sb[:, d, a:b], ALU.mult)
-
-        def half_add(dst, pulled_part, other):
-            nc.vector.scalar_tensor_tensor(dst, pulled_part, 0.5, other, ALU.mult, ALU.add)
-
-        pull(pulled[0][:], 0, 0, cut)
-        pull(pulled[1][:], 1, 0, cut)
-        nc.vector.tensor_tensor(base[:], y[:], own[:], ALU.mult)
-        pull(sq[:, :rest], 0, cut, S)
-        half_add(part[:, :cut], pulled[0][:], base[:, :cut])
-        half_add(part[:, cut:], sq[:, :rest], base[:, cut:])
-        half_add(res[:, :cut], pulled[1][:], part[:, :cut])
-        nc.sync.dma_start(out[:, :cut], res[:, :cut])
-        pull(pulled[0][:, :rest], 1, cut, S)
-        half_add(res[:, cut:], pulled[0][:, :rest], part[:, cut:])
-        nc.scalar.dma_start(out[:, cut:], res[:, cut:])
+        for d in range(2):
+            for a, b in HALVES:
+                nc.vector.tensor_tensor(
+                    pulled[d][:, a:b], y[:].indirect(pos_sb[d][:, a // LANE : b // LANE]), gate_sb[d][:, a:b], ALU.mult
+                )
+        for a, b in HALVES:
+            nc.vector.tensor_tensor(both[:, a:b], pulled[0][:, a:b], pulled[1][:, a:b], ALU.add)
+        for a, b in HALVES:
+            nc.vector.tensor_tensor(base[:, a:b], y[:, a:b], own[:, a:b], ALU.mult)
+        for a, b in CHUNKS:
+            nc.vector.scalar_tensor_tensor(res[:, a:b], both[:, a:b], 0.5, base[:, a:b], ALU.mult, ALU.add)
+            (nc.scalar if a == 384 else nc.sync).dma_start(out[:, a:b], res[:, a:b])

@@ -114,25 +114,30 @@ def tile_picked_ygread_zeld_p_kernel(tc, x_words, x_scales, w1, gate, rate, offs
 
         sq = keep.tile([P, S], F32, name="sq")
         own = keep.tile([P, S], F32, name="own")
-        for a, b in HALVES:
-            nc.scalar.activation(sq[:, a:b], y[:, a:b], ACT.Square, bias=-0.5)
-        for a, b in HALVES:
-            nc.scalar.activation(own[:, a:b], sq[:, a:b], ACT.Identity, scale=coef[:, 0:1], bias=coef[:, 1:2])
+        nc.scalar.activation(sq[:], y[:], ACT.Square, bias=-0.5)
+        nc.scalar.activation(own[:], sq[:], ACT.Identity, scale=coef[:, 0:1], bias=coef[:, 1:2])
 
-        pulled = [keep.tile([P, S], F32, name=f"pulled{d}") for d in range(2)]
-        both = keep.tile([P, S], F32, name="both")
+        cut = 384
+        rest = S - cut
+        pulled = [keep.tile([P, cut], F32, name=f"pulled{d}") for d in range(2)]
         base = keep.tile([P, S], F32, name="base")
+        part = keep.tile([P, S], F32, name="part")
         res = keep.tile([P, S], F32, name="res")
 
-        for d in range(2):
-            for a, b in HALVES:
-                nc.vector.tensor_tensor(
-                    pulled[d][:, a:b], y[:].indirect(pos_sb[d][:, a // LANE : b // LANE]), gate_sb[d][:, a:b], ALU.mult
-                )
-        for a, b in HALVES:
-            nc.vector.tensor_tensor(both[:, a:b], pulled[0][:, a:b], pulled[1][:, a:b], ALU.add)
-        for a, b in HALVES:
-            nc.vector.tensor_tensor(base[:, a:b], y[:, a:b], own[:, a:b], ALU.mult)
-        for a, b in CHUNKS:
-            nc.vector.scalar_tensor_tensor(res[:, a:b], both[:, a:b], 0.5, base[:, a:b], ALU.mult, ALU.add)
-            (nc.scalar if a == 384 else nc.sync).dma_start(out[:, a:b], res[:, a:b])
+        def pull(dst, d, a, b):
+            nc.vector.tensor_tensor(dst, y[:].indirect(pos_sb[d][:, a // LANE : b // LANE]), gate_sb[d][:, a:b], ALU.mult)
+
+        def half_add(dst, pulled_part, other):
+            nc.vector.scalar_tensor_tensor(dst, pulled_part, 0.5, other, ALU.mult, ALU.add)
+
+        pull(pulled[0][:], 0, 0, cut)
+        pull(pulled[1][:], 1, 0, cut)
+        nc.vector.tensor_tensor(base[:], y[:], own[:], ALU.mult)
+        pull(sq[:, :rest], 0, cut, S)
+        half_add(part[:, :cut], pulled[0][:], base[:, :cut])
+        half_add(part[:, cut:], sq[:, :rest], base[:, cut:])
+        half_add(res[:, :cut], pulled[1][:], part[:, :cut])
+        nc.sync.dma_start(out[:, :cut], res[:, :cut])
+        pull(pulled[0][:, :rest], 1, cut, S)
+        half_add(res[:, cut:], pulled[0][:, :rest], part[:, cut:])
+        nc.scalar.dma_start(out[:, cut:], res[:, cut:])

@@ -27,54 +27,59 @@ def tile_picked_ygread_zeld_p_kernel(tc, x_words, x_scales, w1, gate, rate, offs
     nc = tc.nc
     with ExitStack() as ctx:
         keep = ctx.enter_context(tc.tile_pool(name="keep", bufs=1))
+        late = ctx.enter_context(tc.tile_pool(name="late", bufs=1))
         psum = ctx.enter_context(tc.psum_pool(name="psum", bufs=1))
 
         offs_sb = keep.tile([P, S // LANE], U16, name="offs_sb")
         pos_sb = [keep.tile([P, S // LANE], U16, name=f"pos_sb{d}") for d in range(2)]
-        words = [keep.tile([P, T], U32, name=f"words{g}", align_bytes=64) for g in range(PASSES)]
+        words = [keep.tile([P, T], U32, name=f"words{g}", tag=f"words{g}", align_bytes=64) for g in range(PASSES)]
         scales = keep.tile([P, T], U8, name="scales", align_bytes=64)
         w_raw = [keep.tile([P, PACK, M], F32, name=f"w_raw{g}", tag=f"w_raw{g}", align_bytes=64) for g in range(PASSES)]
-        gate_sb = [keep.tile([P, S], F32, name=f"gate_sb{d}") for d in range(2)]
-        rate_sb = keep.tile([P, 1], F32, name="rate_sb")
+        picked_rows = late.tile([P, S], U8, name="picked_rows", offset=0)
+        rate_sb = late.tile([P, 1], F32, name="rate_sb", offset=0)
 
-        nc.vector.memset(scales[:].bitcast(I32), 0)
+        picked_scales = keep.tile([P, PASSES * S], U8, name="picked_scales", align_bytes=64)
+        nc.vector.memset(scales[32:64, :].bitcast(I32), 0)
+        nc.vector.memset(scales[64:P, :].bitcast(I32), 0)
+        nc.vector.memset(picked_scales[:].bitcast(I32), 0)
         warm = keep.tile([P, 2], F32, name="warm")
         nc.vector.memset(warm[:, 0:1], 0.0)
         nc.scalar.activation(warm[:, 1:2], warm[:, 0:1], ACT.Sigmoid)
 
         def load_words(g):
-            nc.sync.dma_start(words[g][:].bitcast(I32), x_words[g].rearrange("p c r -> p (c r)").bitcast(I32))
+            rows = x_words.rearrange("o (b g i) c r -> g (o b) i (c r)", g=PASSES, i=8)
+            nc.sync.dma_start(words[g][:].bitcast(I32), rows[g].bitcast(I32))
 
         def load_weights(g):
-            nc.sync.dma_start(w_raw[g][:], w1[512 * g : 512 * (g + 1), :].rearrange("(p j) m -> p j m", j=PACK))
+            rows = w1.rearrange("(b g i j) m -> g b i (j m)", g=PASSES, i=8, j=PACK)
+            nc.sync.dma_start(w_raw[g][:].rearrange("p j m -> p (j m)"), rows[g])
 
         nc.sync.dma_start(offs_sb[:], offs)
+        nc.sync.dma_start(scales[0:32, :].bitcast(I32), x_scales.rearrange("o q c -> (o q) c").bitcast(I32))
         load_words(0)
-        for q in range(4):
-            nc.sync.dma_start(
-                scales[32 * q : 32 * q + 8, :].bitcast(I32),
-                x_scales[:, 4 * q : 4 * q + 4, :].bitcast(I32),
-            )
         load_weights(0)
         load_weights(1)
         load_words(1)
         nc.sync.dma_start(pos_sb[0][:], pos1)
-        nc.sync.dma_start(gate_sb[0][:], gate[0])
-        nc.sync.dma_start(rate_sb[:], rate)
         nc.sync.dma_start(pos_sb[1][:], pos2)
-        nc.sync.dma_start(gate_sb[1][:], gate[1])
 
-        w_bf = keep.tile([P, PASSES * M * PACK], BF16, name="w_bf", align_bytes=64)
+        nc.vector.tensor_copy(picked_rows[:], scales[:].indirect(offs_sb[:]))
+        for q in range(4):
+            nc.sync.dma_start(
+                picked_scales[32 * q : 32 * q + 4, :].bitcast(I32), picked_rows[8 * q : 8 * q + 8, :].bitcast(I32)
+            )
+        nc.sync.dma_start(rate_sb[:], rate)
+
+        w_bf = keep.tile([P, PASSES * M * PACK], BF16, name="w_bf", tag="w_bf", align_bytes=64)
+
+        picked = [keep.tile([P, S], U32, name="picked0", align_bytes=64)]
+        nc.vector.tensor_copy(picked[0][:], words[0][:].indirect(offs_sb[:]))
+
         for g in range(PASSES):
             nc.scalar.copy(
                 w_bf[:, g * M * PACK : (g + 1) * M * PACK].rearrange("p (m j) -> p m j", j=PACK),
                 w_raw[g][:].rearrange("p j m -> p m j"),
             )
-
-        picked = [keep.tile([P, S], U32, name="picked0", align_bytes=64)]
-        picked_scales = keep.tile([P, S], U8, name="picked_scales", align_bytes=64)
-        nc.vector.tensor_copy(picked[0][:], words[0][:].indirect(offs_sb[:]))
-        nc.vector.tensor_copy(picked_scales[:], scales[:].indirect(offs_sb[:]))
 
         w_codes = keep.tile([P, PASSES * M], U32, name="w_codes", align_bytes=64)
         w_scales = keep.tile([P, PASSES * M], U8, name="w_scales", align_bytes=64)
@@ -84,6 +89,13 @@ def tile_picked_ygread_zeld_p_kernel(tc, x_words, x_scales, w1, gate, rate, offs
                 scales=w_scales[:, g * M : (g + 1) * M],
                 in_=w_bf[:, g * M * PACK : (g + 1) * M * PACK],
             )
+
+        gate_sb = [
+            keep.tile([P, S], F32, name=f"gate_sb{d}", tag=tag, align_bytes=64)
+            for d, tag in enumerate(("w_raw0", "w_bf"))
+        ]
+        for d in range(2):
+            nc.sync.dma_start(gate_sb[d][:], gate[d])
 
         picked.append(keep.tile([P, S], U32, name="picked1", tag="w_raw1", align_bytes=64))
         y = keep.tile([P, S], F32, name="y")
@@ -96,7 +108,7 @@ def tile_picked_ygread_zeld_p_kernel(tc, x_words, x_scales, w1, gate, rate, offs
                 lhsT=w_codes[:, g * M : (g + 1) * M].bitcast(FP8X4),
                 lhsT_scale=w_scales[:, g * M : (g + 1) * M],
                 rhs=picked[g][:, a:b].bitcast(FP8X4),
-                rhs_scale=picked_scales[4 * g : P, a:b],
+                rhs_scale=picked_scales[:, g * S + a : g * S + b],
                 start=(g == 0),
                 stop=(g == PASSES - 1),
             )

@@ -47,15 +47,14 @@ def tile_picked_ygread_zeld_p_kernel(tc, x_words, x_scales, w1, gate, rate, offs
         nc.scalar.activation(warm[:, 1:2], warm[:, 0:1], ACT.Sigmoid)
 
         def load_words(g):
-            rows = x_words.rearrange("o (b g i) c r -> g (o b) i (c r)", g=PASSES, i=8)
-            nc.sync.dma_start(words[g][:].bitcast(I32), rows[g].bitcast(I32))
+            nc.sync.dma_start(words[g][:].bitcast(I32), x_words[g].rearrange("p c r -> p (c r)").bitcast(I32))
 
         def load_weights(g):
-            rows = w1.rearrange("(b g i j) m -> g b i (j m)", g=PASSES, i=8, j=PACK)
-            nc.sync.dma_start(w_raw[g][:].rearrange("p j m -> p (j m)"), rows[g])
+            nc.sync.dma_start(w_raw[g][:], w1[512 * g : 512 * (g + 1), :].rearrange("(p j) m -> p j m", j=PACK))
 
         nc.sync.dma_start(offs_sb[:], offs)
-        nc.sync.dma_start(scales[0:32, :].bitcast(I32), x_scales.rearrange("o q c -> (o q) c").bitcast(I32))
+        for g, queue in enumerate((nc.scalar, nc.sync)):
+            queue.dma_start(scales[g:32:PASSES, :].bitcast(I32), x_scales[g].bitcast(I32))
         load_words(0)
         load_weights(0)
         load_weights(1)

@@ -16,95 +16,110 @@ ACT = mybir.ActivationFunctionType
 ALU = mybir.AluOpType
 
 P = 128
+QUAD = 32
 PACK = 4
-PASSES = 2
+PASSES = K // (P * PACK)
+ROWS = 4
 LANE = 16
-CHUNKS = ((0, 256), (256, 384), (384, 512))
-HALVES = ((0, 256), (256, 512))
+ALIGN = 64
+STRETCHES = ((0, 256), (256, 384), (384, 512))
+CUT = 384
 
 
 def tile_picked_ygread_zeld_p_kernel(tc, x_words, x_scales, w1, gate, rate, offs, pos1, pos2, out):
     nc = tc.nc
     with ExitStack() as ctx:
         keep = ctx.enter_context(tc.tile_pool(name="keep", bufs=1))
-        late = ctx.enter_context(tc.tile_pool(name="late", bufs=1))
+        reused = ctx.enter_context(tc.tile_pool(name="reused", bufs=1))
         psum = ctx.enter_context(tc.psum_pool(name="psum", bufs=1))
+
+        codes1_at = 0
+        rate_at = codes1_at + M * PACK
+        picked1_at = rate_at + ALIGN
+        raw0_at = rate_at - ALIGN
 
         offs_sb = keep.tile([P, S // LANE], U16, name="offs_sb")
         pos_sb = [keep.tile([P, S // LANE], U16, name=f"pos_sb{d}") for d in range(2)]
-        words = [keep.tile([P, T], U32, name=f"words{g}", tag=f"words{g}", align_bytes=64) for g in range(PASSES)]
-        scales = keep.tile([P, T], U8, name="scales", align_bytes=64)
-        w_raw = [keep.tile([P, PACK, M], F32, name=f"w_raw{g}", tag=f"w_raw{g}", align_bytes=64) for g in range(PASSES)]
-        picked_rows = late.tile([P, S], U8, name="picked_rows", offset=0)
-        rate_sb = late.tile([P, 1], F32, name="rate_sb", offset=0)
+        words = [keep.tile([P, T], U32, name=f"words{g}", align_bytes=ALIGN) for g in range(PASSES)]
+        scale_rows = keep.tile([P, T], U8, name="scale_rows", align_bytes=ALIGN)
+        w_raw = [
+            reused.tile([P, PACK, M], F32, name="w_raw0", offset=raw0_at, align_bytes=ALIGN),
+            keep.tile([P, PACK, M], F32, name="w_raw1", tag="w_raw1", align_bytes=ALIGN),
+        ]
+        picked_rows = keep.tile([P, S], U8, name="picked_rows")
+        picked_scales = keep.tile([P, PASSES * S], U8, name="picked_scales", align_bytes=ALIGN)
 
-        picked_scales = keep.tile([P, PASSES * S], U8, name="picked_scales", align_bytes=64)
-        nc.vector.memset(scales[32:64, :].bitcast(I32), 0)
-        nc.vector.memset(scales[64:P, :].bitcast(I32), 0)
+        half = keep.tile([P, 2], F32, name="half")
+        nc.vector.memset(half[:, 0:1], 0.0)
+        nc.scalar.activation(half[:, 1:2], half[:, 0:1], ACT.Sigmoid)
+
+        nc.vector.memset(scale_rows[QUAD : 2 * QUAD, :].bitcast(I32), 0)
+        nc.vector.memset(scale_rows[2 * QUAD : P, :].bitcast(I32), 0)
         nc.vector.memset(picked_scales[:].bitcast(I32), 0)
-        warm = keep.tile([P, 2], F32, name="warm")
-        nc.vector.memset(warm[:, 0:1], 0.0)
-        nc.scalar.activation(warm[:, 1:2], warm[:, 0:1], ACT.Sigmoid)
+
+        nc.sync.dma_start(offs_sb[:], offs)
+        for g, queue in enumerate((nc.scalar, nc.sync)):
+            queue.dma_start(scale_rows[g:QUAD:PASSES, :].bitcast(I32), x_scales[g].bitcast(I32))
 
         def load_words(g):
             nc.sync.dma_start(words[g][:].bitcast(I32), x_words[g].rearrange("p c r -> p (c r)").bitcast(I32))
 
-        def load_weights(g):
-            nc.sync.dma_start(w_raw[g][:], w1[512 * g : 512 * (g + 1), :].rearrange("(p j) m -> p j m", j=PACK))
-
-        nc.sync.dma_start(offs_sb[:], offs)
-        for g, queue in enumerate((nc.scalar, nc.sync)):
-            queue.dma_start(scales[g:32:PASSES, :].bitcast(I32), x_scales[g].bitcast(I32))
         load_words(0)
-        load_weights(0)
-        load_weights(1)
+        for g in range(PASSES):
+            k_rows = w1[P * PACK * g : P * PACK * (g + 1), :]
+            nc.sync.dma_start(w_raw[g][:], k_rows.rearrange("(p t) m -> p t m", t=PACK))
         load_words(1)
         nc.sync.dma_start(pos_sb[0][:], pos1)
         nc.sync.dma_start(pos_sb[1][:], pos2)
 
-        nc.vector.tensor_copy(picked_rows[:], scales[:].indirect(offs_sb[:]))
-        for q in range(4):
-            nc.sync.dma_start(
-                picked_scales[32 * q : 32 * q + 4, :].bitcast(I32), picked_rows[8 * q : 8 * q + 8, :].bitcast(I32)
-            )
-        nc.sync.dma_start(rate_sb[:], rate)
-
-        w_bf = keep.tile([P, PASSES * M * PACK], BF16, name="w_bf", tag="w_bf", align_bytes=64)
-
-        picked = [keep.tile([P, S], U32, name="picked0", align_bytes=64)]
-        nc.vector.tensor_copy(picked[0][:], words[0][:].indirect(offs_sb[:]))
-
-        for g in range(PASSES):
-            nc.scalar.copy(
-                w_bf[:, g * M * PACK : (g + 1) * M * PACK].rearrange("p (m j) -> p m j", j=PACK),
-                w_raw[g][:].rearrange("p j m -> p m j"),
+        nc.vector.tensor_copy(picked_rows[:], scale_rows[:].indirect(offs_sb[:]))
+        for q in range(P // QUAD):
+            nc.scalar.dma_start(
+                picked_scales[QUAD * q : QUAD * q + ROWS, :].bitcast(I32),
+                picked_rows[PASSES * ROWS * q : PASSES * ROWS * (q + 1), :].bitcast(I32),
             )
 
-        w_codes = keep.tile([P, PASSES * M], U32, name="w_codes", align_bytes=64)
-        w_scales = keep.tile([P, PASSES * M], U8, name="w_scales", align_bytes=64)
+        picked0 = keep.tile([P, S], U32, name="picked0", align_bytes=ALIGN)
+        nc.vector.tensor_copy(picked0[:], words[0][:].indirect(offs_sb[:]))
+
+        w_bf = keep.tile([P, PASSES * M * PACK], BF16, name="w_bf", tag="w_bf", align_bytes=ALIGN)
+        for g, cast in enumerate((nc.scalar.copy, nc.vector.tensor_copy)):
+            cast(
+                w_bf[:, g * M * PACK : (g + 1) * M * PACK].rearrange("p (m t) -> p m t", t=PACK),
+                w_raw[g][:].rearrange("p t m -> p m t"),
+            )
+
+        w_codes = [
+            keep.tile([P, M], U32, name="w_codes0", align_bytes=ALIGN),
+            reused.tile([P, M], U32, name="w_codes1", offset=codes1_at, align_bytes=ALIGN),
+        ]
+        w_scales = keep.tile([P, PASSES * M], U8, name="w_scales", align_bytes=ALIGN)
         for g in range(PASSES):
             nc.vector.quantize_mx(
-                out=w_codes[:, g * M : (g + 1) * M].bitcast(FP8X4),
+                out=w_codes[g][:].bitcast(FP8X4),
                 scales=w_scales[:, g * M : (g + 1) * M],
                 in_=w_bf[:, g * M * PACK : (g + 1) * M * PACK],
             )
 
+        rate_sb = reused.tile([P, 1], F32, name="rate_sb", offset=rate_at, align_bytes=ALIGN)
+        nc.sync.dma_start(rate_sb[:], rate)
         gate_sb = [
-            keep.tile([P, S], F32, name=f"gate_sb{d}", tag=tag, align_bytes=64)
-            for d, tag in enumerate(("w_raw0", "w_bf"))
+            keep.tile([P, S], F32, name=f"gate_sb{d}", tag=tag, align_bytes=ALIGN)
+            for d, tag in enumerate(("w_raw1", "w_bf"))
         ]
         for d in range(2):
             nc.sync.dma_start(gate_sb[d][:], gate[d])
 
-        picked.append(keep.tile([P, S], U32, name="picked1", tag="w_raw1", align_bytes=64))
+        picked1 = reused.tile([P, S], U32, name="picked1", offset=picked1_at, align_bytes=ALIGN)
+        picked = (picked0, picked1)
         y = keep.tile([P, S], F32, name="y")
-        acc = [psum.tile([P, b - a], F32, name=f"acc{a}") for a, b in CHUNKS]
+        acc = [psum.tile([P, b - a], F32, name=f"acc{a}") for a, b in STRETCHES]
 
         def product(c, g):
-            a, b = CHUNKS[c]
+            a, b = STRETCHES[c]
             nc.tensor.matmul_mx(
                 out=acc[c][:],
-                lhsT=w_codes[:, g * M : (g + 1) * M].bitcast(FP8X4),
+                lhsT=w_codes[g][:].bitcast(FP8X4),
                 lhsT_scale=w_scales[:, g * M : (g + 1) * M],
                 rhs=picked[g][:, a:b].bitcast(FP8X4),
                 rhs_scale=picked_scales[:, g * S + a : g * S + b],
@@ -112,25 +127,23 @@ def tile_picked_ygread_zeld_p_kernel(tc, x_words, x_scales, w1, gate, rate, offs
                 stop=(g == PASSES - 1),
             )
 
-        for c in range(len(CHUNKS)):
+        for c in range(len(STRETCHES)):
             product(c, 0)
-        for c, (a, b) in enumerate(CHUNKS):
-            nc.vector.tensor_copy(picked[1][:, a:b], words[1][:].indirect(offs_sb[:, a // LANE : b // LANE]))
+        for c, (a, b) in enumerate(STRETCHES):
+            nc.vector.tensor_copy(picked1[:, a:b], words[1][:].indirect(offs_sb[:, a // LANE : b // LANE]))
             product(c, 1)
             nc.scalar.activation(y[:, a:b], acc[c][:], ACT.Sigmoid)
 
         coef = keep.tile([P, 2], F32, name="coef")
         nc.scalar.activation(coef[:, 0:1], rate_sb[:], ACT.Copy, scale=-1.0)
         nc.scalar.activation(coef[:, 1:2], rate_sb[:], ACT.Copy, scale=0.25, bias=0.5)
-
         sq = keep.tile([P, S], F32, name="sq")
         own = keep.tile([P, S], F32, name="own")
-        nc.scalar.activation(sq[:], y[:], ACT.Square, bias=-0.5)
+        nc.scalar.activation(sq[:], y[:], ACT.Square, scale=-1.0, bias=half[:, 1:2])
         nc.scalar.activation(own[:], sq[:], ACT.Identity, scale=coef[:, 0:1], bias=coef[:, 1:2])
 
-        cut = 384
-        rest = S - cut
-        pulled = [keep.tile([P, cut], F32, name=f"pulled{d}") for d in range(2)]
+        rest = S - CUT
+        pulled = [keep.tile([P, CUT], F32, name=f"pulled{d}") for d in range(2)]
         base = keep.tile([P, S], F32, name="base")
         part = keep.tile([P, S], F32, name="part")
         res = keep.tile([P, S], F32, name="res")
@@ -141,14 +154,14 @@ def tile_picked_ygread_zeld_p_kernel(tc, x_words, x_scales, w1, gate, rate, offs
         def half_add(dst, pulled_part, other):
             nc.vector.scalar_tensor_tensor(dst, pulled_part, 0.5, other, ALU.mult, ALU.add)
 
-        pull(pulled[0][:], 0, 0, cut)
-        pull(pulled[1][:], 1, 0, cut)
+        pull(pulled[0][:], 0, 0, CUT)
+        pull(pulled[1][:], 1, 0, CUT)
         nc.vector.tensor_tensor(base[:], y[:], own[:], ALU.mult)
-        pull(sq[:, :rest], 0, cut, S)
-        half_add(part[:, :cut], pulled[0][:], base[:, :cut])
-        half_add(part[:, cut:], sq[:, :rest], base[:, cut:])
-        half_add(res[:, :cut], pulled[1][:], part[:, :cut])
-        nc.sync.dma_start(out[:, :cut], res[:, :cut])
-        pull(pulled[0][:, :rest], 1, cut, S)
-        half_add(res[:, cut:], pulled[0][:, :rest], part[:, cut:])
-        nc.scalar.dma_start(out[:, cut:], res[:, cut:])
+        pull(sq[:, :rest], 0, CUT, S)
+        half_add(part[:, :CUT], pulled[0][:], base[:, :CUT])
+        half_add(part[:, CUT:], sq[:, :rest], base[:, CUT:])
+        half_add(res[:, :CUT], pulled[1][:], part[:, :CUT])
+        nc.sync.dma_start(out[:, :CUT], res[:, :CUT])
+        pull(pulled[0][:, :rest], 1, CUT, S)
+        half_add(res[:, CUT:], pulled[0][:, :rest], part[:, CUT:])
+        nc.scalar.dma_start(out[:, CUT:], res[:, CUT:])

@@ -1,6 +1,7 @@
 from contextlib import ExitStack
 
 import concourse.mybir as mybir
+from concourse.masks import make_identity
 
 K, T, S, M = 1024, 1024, 512, 128
 FLOPS = 2 * K * M * S
@@ -52,6 +53,9 @@ def tile_picked_ygread_zeld_p_kernel(tc, x_words, x_scales, w1, gate, rate, offs
         half = keep.tile([P, 2], F32, name="half")
         nc.vector.memset(half[:, 0:1], 0.0)
         nc.scalar.activation(half[:, 1:2], half[:, 0:1], ACT.Sigmoid)
+
+        ident = keep.tile([P, P], F32, name="ident")
+        make_identity(nc, ident[:])
 
         nc.vector.memset(scale_rows[QUAD : 2 * QUAD, :].bitcast(I32), 0)
         nc.vector.memset(scale_rows[2 * QUAD : P, :].bitcast(I32), 0)
@@ -113,7 +117,7 @@ def tile_picked_ygread_zeld_p_kernel(tc, x_words, x_scales, w1, gate, rate, offs
         picked1 = reused.tile([P, S], U32, name="picked1", offset=picked1_at, align_bytes=ALIGN)
         picked = (picked0, picked1)
         y = keep.tile([P, S], F32, name="y")
-        acc = [psum.tile([P, b - a], F32, name=f"acc{a}") for a, b in STRETCHES]
+        acc = [psum.tile([P, b - a], F32, name=f"acc{a}", tag=f"acc{a}") for a, b in STRETCHES]
 
         def product(c, g):
             a, b = STRETCHES[c]
@@ -134,34 +138,56 @@ def tile_picked_ygread_zeld_p_kernel(tc, x_words, x_scales, w1, gate, rate, offs
             product(c, 1)
             nc.scalar.activation(y[:, a:b], acc[c][:], ACT.Sigmoid)
 
-        coef = keep.tile([P, 2], F32, name="coef")
-        nc.scalar.activation(coef[:, 0:1], rate_sb[:], ACT.Copy, scale=-1.0)
-        nc.scalar.activation(coef[:, 1:2], rate_sb[:], ACT.Copy, scale=0.25, bias=0.5)
-        sq = keep.tile([P, S], F32, name="sq")
-        own = keep.tile([P, S], F32, name="own")
-        nc.scalar.activation(sq[:], y[:], ACT.Square, scale=-1.0, bias=half[:, 1:2])
-        nc.scalar.activation(own[:], sq[:], ACT.Identity, scale=coef[:, 0:1], bias=coef[:, 1:2])
-
-        rest = S - CUT
-        pulled = [keep.tile([P, CUT], F32, name=f"pulled{d}") for d in range(2)]
-        base = keep.tile([P, S], F32, name="base")
-        part = keep.tile([P, S], F32, name="part")
-        res = keep.tile([P, S], F32, name="res")
+        coef = keep.tile([P, 4], F32, name="coef")
+        nc.scalar.activation(coef[:, 0:1], rate_sb[:], ACT.Copy, scale=-2.0)
+        nc.scalar.activation(coef[:, 1:2], rate_sb[:], ACT.Copy, scale=0.5, bias=1.0)
+        nc.scalar.activation(coef[:, 2:3], rate_sb[:], ACT.Copy, scale=-1.0)
+        nc.scalar.activation(coef[:, 3:4], rate_sb[:], ACT.Copy, scale=0.25, bias=0.5)
+        halves = ((0, S // 2), (S // 2, S))
+        sq = keep.tile([P, S], F32, name="sq", tag="sq")
+        twice = keep.tile([P, S], F32, name="twice")
+        for a, b in halves:
+            nc.scalar.activation(sq[:, a:b], y[:, a:b], ACT.Square, scale=-1.0, bias=half[:, 1:2])
+        thirds = ((0, S // 2), (S // 2, CUT), (CUT, S))
+        for a, b in thirds:
+            c = 0 if a < CUT else 2
+            nc.scalar.activation(twice[:, a:b], sq[:, a:b], ACT.Identity, scale=coef[:, c : c + 1], bias=coef[:, c + 1 : c + 2])
 
         def pull(dst, d, a, b):
-            nc.vector.tensor_tensor(dst, y[:].indirect(pos_sb[d][:, a // LANE : b // LANE]), gate_sb[d][:, a:b], ALU.mult)
+            nc.vector.tensor_tensor(dst[:, a:b], y[:].indirect(pos_sb[d][:, a // LANE : b // LANE]), gate_sb[d][:, a:b], ALU.mult)
 
-        def half_add(dst, pulled_part, other):
-            nc.vector.scalar_tensor_tensor(dst, pulled_part, 0.5, other, ALU.mult, ALU.add)
+        pulled0 = keep.tile([P, S], F32, name="pulled0")
+        base = keep.tile([P, S], F32, name="base")
+        blocks = CUT // P
+        turned = [psum.tile([P, P], F32, name=f"turned{i}") for i in range(blocks)]
+        turned_sb = keep.tile([P, CUT], F32, name="turned_sb")
+        ends = ((0, S // 2), (S // 2, CUT))
+        back = [psum.tile([P, b - a], F32, name=f"back{h}", tag=f"acc{STRETCHES[h][0]}") for h, (a, b) in enumerate(ends)]
+        part = keep.tile([P, S - CUT], F32, name="part")
+        res = keep.tile([P, S], F32, name="res")
 
-        pull(pulled[0][:], 0, 0, CUT)
-        pull(pulled[1][:], 1, 0, CUT)
-        nc.vector.tensor_tensor(base[:], y[:], own[:], ALU.mult)
-        pull(sq[:, :rest], 0, CUT, S)
-        half_add(part[:, :CUT], pulled[0][:], base[:, :CUT])
-        half_add(part[:, CUT:], sq[:, :rest], base[:, CUT:])
-        half_add(res[:, :CUT], pulled[1][:], part[:, :CUT])
-        nc.sync.dma_start(out[:, :CUT], res[:, :CUT])
-        pull(pulled[0][:, :rest], 1, CUT, S)
-        half_add(res[:, CUT:], pulled[0][:, :rest], part[:, CUT:])
-        nc.scalar.dma_start(out[:, CUT:], res[:, CUT:])
+        def turn(dst, src, start, stop):
+            nc.tensor.matmul(dst, src, ident[:], start=start, stop=stop, is_transpose=True)
+
+        for a, b in halves:
+            pull(pulled0, 0, a, b)
+            for i in range(a // P, min(b, CUT) // P):
+                turn(turned[i][:], pulled0[:, i * P : (i + 1) * P], True, False)
+        for a, b in thirds:
+            nc.vector.tensor_tensor(base[:, a:b], y[:, a:b], twice[:, a:b], ALU.mult)
+            for i in range(a // P, min(b, CUT) // P):
+                turn(turned[i][:], base[:, i * P : (i + 1) * P], False, True)
+        for h, (a, b) in enumerate(ends):
+            for i in range(a // P, b // P):
+                nc.scalar.activation(turned_sb[:, i * P : (i + 1) * P], turned[i][:], ACT.Copy, scale=0.5)
+                turn(back[h][:, i * P - a : (i + 1) * P - a], turned_sb[:, i * P : (i + 1) * P], True, True)
+        pulled1 = keep.tile([P, S], F32, name="pulled1", tag="sq")
+        pull(pulled1, 1, CUT, S)
+        nc.vector.scalar_tensor_tensor(part[:], pulled0[:, CUT:], 0.5, base[:, CUT:], ALU.mult, ALU.add)
+        pull(pulled1, 1, *ends[0])
+        nc.vector.scalar_tensor_tensor(res[:, CUT:], pulled1[:, CUT:], 0.5, part[:], ALU.mult, ALU.add)
+        nc.sync.dma_start(out[:, CUT:], res[:, CUT:])
+        pull(pulled1, 1, *ends[1])
+        for h, (a, b) in enumerate(ends):
+            nc.vector.scalar_tensor_tensor(res[:, a:b], pulled1[:, a:b], 0.5, back[h][:], ALU.mult, ALU.add)
+            (nc.sync, nc.scalar)[h].dma_start(out[:, a:b], res[:, a:b])

@@ -25,6 +25,8 @@ LANE = 16
 ALIGN = 64
 STRETCHES = ((0, 256), (256, 384), (384, 512))
 CUT = 384
+HALVES = ((0, S // 2), (S // 2, S))
+TURNED_PIECES = ((0, S // 2), (S // 2, CUT))
 
 
 def tile_picked_ygread_zeld_p_kernel(tc, x_words, x_scales, w1, gate, rate, offs, pos1, pos2, out):
@@ -78,7 +80,7 @@ def tile_picked_ygread_zeld_p_kernel(tc, x_words, x_scales, w1, gate, rate, offs
 
         nc.vector.tensor_copy(picked_rows[:], scale_rows[:].indirect(offs_sb[:]))
         for q in range(P // QUAD):
-            nc.scalar.dma_start(
+            (nc.scalar, nc.sync)[q % 2].dma_start(
                 picked_scales[QUAD * q : QUAD * q + ROWS, :].bitcast(I32),
                 picked_rows[PASSES * ROWS * q : PASSES * ROWS * (q + 1), :].bitcast(I32),
             )
@@ -131,63 +133,68 @@ def tile_picked_ygread_zeld_p_kernel(tc, x_words, x_scales, w1, gate, rate, offs
                 stop=(g == PASSES - 1),
             )
 
-        for c in range(len(STRETCHES)):
-            product(c, 0)
         for c, (a, b) in enumerate(STRETCHES):
             nc.vector.tensor_copy(picked1[:, a:b], words[1][:].indirect(offs_sb[:, a // LANE : b // LANE]))
+            product(c, 0)
             product(c, 1)
             nc.scalar.activation(y[:, a:b], acc[c][:], ACT.Sigmoid)
 
-        coef = keep.tile([P, 4], F32, name="coef")
+        coef = keep.tile([P, 2], F32, name="coef")
         nc.scalar.activation(coef[:, 0:1], rate_sb[:], ACT.Copy, scale=-2.0)
         nc.scalar.activation(coef[:, 1:2], rate_sb[:], ACT.Copy, scale=0.5, bias=1.0)
-        nc.scalar.activation(coef[:, 2:3], rate_sb[:], ACT.Copy, scale=-1.0)
-        nc.scalar.activation(coef[:, 3:4], rate_sb[:], ACT.Copy, scale=0.25, bias=0.5)
-        halves = ((0, S // 2), (S // 2, S))
         sq = keep.tile([P, S], F32, name="sq", tag="sq")
-        twice = keep.tile([P, S], F32, name="twice")
-        for a, b in halves:
+        factor = keep.tile([P, S], F32, name="factor")
+        for a, b in HALVES:
             nc.scalar.activation(sq[:, a:b], y[:, a:b], ACT.Square, scale=-1.0, bias=half[:, 1:2])
-        thirds = ((0, S // 2), (S // 2, CUT), (CUT, S))
-        for a, b in thirds:
-            c = 0 if a < CUT else 2
-            nc.scalar.activation(twice[:, a:b], sq[:, a:b], ACT.Identity, scale=coef[:, c : c + 1], bias=coef[:, c + 1 : c + 2])
+        for a, b in HALVES:
+            nc.scalar.activation(factor[:, a:b], sq[:, a:b], ACT.Identity, scale=coef[:, 0:1], bias=coef[:, 1:2])
 
         def pull(dst, d, a, b):
-            nc.vector.tensor_tensor(dst[:, a:b], y[:].indirect(pos_sb[d][:, a // LANE : b // LANE]), gate_sb[d][:, a:b], ALU.mult)
-
-        pulled0 = keep.tile([P, S], F32, name="pulled0")
-        base = keep.tile([P, S], F32, name="base")
-        blocks = CUT // P
-        turned = [psum.tile([P, P], F32, name=f"turned{i}") for i in range(blocks)]
-        turned_sb = keep.tile([P, CUT], F32, name="turned_sb")
-        ends = ((0, S // 2), (S // 2, CUT))
-        back = [psum.tile([P, b - a], F32, name=f"back{h}", tag=f"acc{STRETCHES[h][0]}") for h, (a, b) in enumerate(ends)]
-        part = keep.tile([P, S - CUT], F32, name="part")
-        res = keep.tile([P, S], F32, name="res")
+            offsets = pos_sb[d][:, a // LANE : b // LANE]
+            nc.vector.tensor_tensor(dst[:, a:b], y[:].indirect(offsets), gate_sb[d][:, a:b], ALU.mult)
 
         def turn(dst, src, start, stop):
             nc.tensor.matmul(dst, src, ident[:], start=start, stop=stop, is_transpose=True)
 
-        for a, b in halves:
+        def half_add(dst, pulled_part, other):
+            nc.vector.scalar_tensor_tensor(dst, pulled_part, 0.5, other, ALU.mult, ALU.add)
+
+        def block(i):
+            return slice(i * P, (i + 1) * P)
+
+        pulled0 = keep.tile([P, S], F32, name="pulled0")
+        own = keep.tile([P, S], F32, name="own")
+        turned = [psum.tile([P, P], F32, name=f"turned{i}") for i in range(CUT // P)]
+        turned_sb = keep.tile([P, CUT], F32, name="turned_sb")
+        back = [
+            psum.tile([P, b - a], F32, name=f"back{h}", tag=f"acc{STRETCHES[h][0]}")
+            for h, (a, b) in enumerate(TURNED_PIECES)
+        ]
+        part = keep.tile([P, S - CUT], F32, name="part")
+        res = keep.tile([P, S], F32, name="res")
+
+        for a, b in HALVES:
             pull(pulled0, 0, a, b)
-            for i in range(a // P, min(b, CUT) // P):
-                turn(turned[i][:], pulled0[:, i * P : (i + 1) * P], True, False)
-        for a, b in thirds:
-            nc.vector.tensor_tensor(base[:, a:b], y[:, a:b], twice[:, a:b], ALU.mult)
-            for i in range(a // P, min(b, CUT) // P):
-                turn(turned[i][:], base[:, i * P : (i + 1) * P], False, True)
-        for h, (a, b) in enumerate(ends):
+        for i in range(CUT // P):
+            turn(turned[i][:], pulled0[:, block(i)], True, False)
+        for a, b in TURNED_PIECES:
+            nc.vector.tensor_tensor(own[:, a:b], y[:, a:b], factor[:, a:b], ALU.mult)
             for i in range(a // P, b // P):
-                nc.scalar.activation(turned_sb[:, i * P : (i + 1) * P], turned[i][:], ACT.Copy, scale=0.5)
-                turn(back[h][:, i * P - a : (i + 1) * P - a], turned_sb[:, i * P : (i + 1) * P], True, True)
+                turn(turned[i][:], own[:, block(i)], False, True)
+        nc.vector.scalar_tensor_tensor(own[:, CUT:], factor[:, CUT:], 0.5, y[:, CUT:], ALU.mult, ALU.mult)
+        for h, (a, b) in enumerate(TURNED_PIECES):
+            for i in range(a // P, b // P):
+                nc.scalar.activation(turned_sb[:, block(i)], turned[i][:], ACT.Copy, scale=0.5)
+                turn(back[h][:, block(i - a // P)], turned_sb[:, block(i)], True, True)
+
         pulled1 = keep.tile([P, S], F32, name="pulled1", tag="sq")
         pull(pulled1, 1, CUT, S)
-        nc.vector.scalar_tensor_tensor(part[:], pulled0[:, CUT:], 0.5, base[:, CUT:], ALU.mult, ALU.add)
-        pull(pulled1, 1, *ends[0])
-        nc.vector.scalar_tensor_tensor(res[:, CUT:], pulled1[:, CUT:], 0.5, part[:], ALU.mult, ALU.add)
+        half_add(part[:], pulled0[:, CUT:], own[:, CUT:])
+        pull(pulled1, 1, *TURNED_PIECES[0])
+        half_add(res[:, CUT:], pulled1[:, CUT:], part[:])
         nc.sync.dma_start(out[:, CUT:], res[:, CUT:])
-        pull(pulled1, 1, *ends[1])
-        for h, (a, b) in enumerate(ends):
-            nc.vector.scalar_tensor_tensor(res[:, a:b], pulled1[:, a:b], 0.5, back[h][:], ALU.mult, ALU.add)
-            (nc.sync, nc.scalar)[h].dma_start(out[:, a:b], res[:, a:b])
+        pull(pulled1, 1, *TURNED_PIECES[1])
+        for h, queue in enumerate((nc.sync, nc.scalar)):
+            a, b = TURNED_PIECES[h]
+            half_add(res[:, a:b], pulled1[:, a:b], back[h][:])
+            queue.dma_start(out[:, a:b], res[:, a:b])

@@ -23,10 +23,9 @@ PASSES = K // (P * PACK)
 ROWS = 4
 LANE = 16
 ALIGN = 64
-STRETCHES = ((0, 256), (256, 384), (384, 512))
-CUT = 384
+BLOCKS = S // P
+EARLY = 3
 HALVES = ((0, S // 2), (S // 2, S))
-TURNED_PIECES = ((0, S // 2), (S // 2, CUT))
 
 
 def tile_picked_ygread_zeld_p_kernel(tc, x_words, x_scales, w1, gate, rate, offs, pos1, pos2, out):
@@ -36,21 +35,17 @@ def tile_picked_ygread_zeld_p_kernel(tc, x_words, x_scales, w1, gate, rate, offs
         reused = ctx.enter_context(tc.tile_pool(name="reused", bufs=1))
         psum = ctx.enter_context(tc.psum_pool(name="psum", bufs=1))
 
-        codes1_at = 0
-        rate_at = codes1_at + M * PACK
-        picked1_at = rate_at + ALIGN
-        raw0_at = rate_at - ALIGN
-
         offs_sb = keep.tile([P, S // LANE], U16, name="offs_sb")
         pos_sb = [keep.tile([P, S // LANE], U16, name=f"pos_sb{d}") for d in range(2)]
-        words = [keep.tile([P, T], U32, name=f"words{g}", align_bytes=ALIGN) for g in range(PASSES)]
-        scale_rows = keep.tile([P, T], U8, name="scale_rows", align_bytes=ALIGN)
-        w_raw = [
-            reused.tile([P, PACK, M], F32, name="w_raw0", offset=raw0_at, align_bytes=ALIGN),
-            keep.tile([P, PACK, M], F32, name="w_raw1", tag="w_raw1", align_bytes=ALIGN),
+        words = [
+            reused.tile([P, T], U32, name="words0", offset=0, align_bytes=ALIGN),
+            keep.tile([P, T], U32, name="words1", align_bytes=ALIGN),
         ]
+        scale_rows = keep.tile([P, T], U8, name="scale_rows", align_bytes=ALIGN)
+        w_raw = [keep.tile([P, PACK, M], F32, name=f"w_raw{g}", tag=f"w_raw{g}", align_bytes=ALIGN) for g in range(PASSES)]
         picked_rows = keep.tile([P, S], U8, name="picked_rows")
         picked_scales = keep.tile([P, PASSES * S], U8, name="picked_scales", align_bytes=ALIGN)
+
 
         half = keep.tile([P, 2], F32, name="half")
         nc.vector.memset(half[:, 0:1], 0.0)
@@ -66,88 +61,92 @@ def tile_picked_ygread_zeld_p_kernel(tc, x_words, x_scales, w1, gate, rate, offs
         nc.sync.dma_start(offs_sb[:], offs)
         for g, queue in enumerate((nc.scalar, nc.sync)):
             queue.dma_start(scale_rows[g:QUAD:PASSES, :].bitcast(I32), x_scales[g].bitcast(I32))
-
-        def load_words(g):
-            nc.sync.dma_start(words[g][:].bitcast(I32), x_words[g].rearrange("p c r -> p (c r)").bitcast(I32))
-
-        load_words(0)
         for g in range(PASSES):
             k_rows = w1[P * PACK * g : P * PACK * (g + 1), :]
             nc.sync.dma_start(w_raw[g][:], k_rows.rearrange("(p t) m -> p t m", t=PACK))
-        load_words(1)
+            nc.sync.dma_start(words[g][:].bitcast(I32), x_words[g].rearrange("p c r -> p (c r)").bitcast(I32))
         nc.sync.dma_start(pos_sb[0][:], pos1)
         nc.sync.dma_start(pos_sb[1][:], pos2)
 
+
         nc.vector.tensor_copy(picked_rows[:], scale_rows[:].indirect(offs_sb[:]))
+
+        w_bf = [keep.tile([P, M * PACK], BF16, name=f"w_bf{g}", align_bytes=ALIGN) for g in range(PASSES)]
+        w_codes = [keep.tile([P, M], U32, name=f"w_codes{g}", align_bytes=ALIGN) for g in range(PASSES)]
+        w_scales = keep.tile([P, PASSES * M], U8, name="w_scales", align_bytes=ALIGN)
+
+        def cast(g):
+            nc.scalar.copy(
+                w_bf[g][:].rearrange("p (c i t) -> p c t i", i=PACK, t=PACK),
+                w_raw[g][:].rearrange("p t (c i) -> p c t i", i=PACK),
+            )
+
+        def quantise(g):
+            nc.vector.quantize_mx(
+                out=w_codes[g][:].bitcast(FP8X4), scales=w_scales[:, g * M : (g + 1) * M], in_=w_bf[g][:]
+            )
+
+        cast(0)
         for q in range(P // QUAD):
-            (nc.scalar, nc.sync)[q % 2].dma_start(
+            nc.sync.dma_start(
                 picked_scales[QUAD * q : QUAD * q + ROWS, :].bitcast(I32),
                 picked_rows[PASSES * ROWS * q : PASSES * ROWS * (q + 1), :].bitcast(I32),
             )
-
-        picked0 = keep.tile([P, S], U32, name="picked0", align_bytes=ALIGN)
-        nc.vector.tensor_copy(picked0[:], words[0][:].indirect(offs_sb[:]))
-
-        w_bf = keep.tile([P, PASSES * M * PACK], BF16, name="w_bf", tag="w_bf", align_bytes=ALIGN)
-        for g, cast in enumerate((nc.scalar.copy, nc.vector.tensor_copy)):
-            cast(
-                w_bf[:, g * M * PACK : (g + 1) * M * PACK].rearrange("p (m t) -> p m t", t=PACK),
-                w_raw[g][:].rearrange("p t m -> p m t"),
-            )
-
-        w_codes = [
-            keep.tile([P, M], U32, name="w_codes0", align_bytes=ALIGN),
-            reused.tile([P, M], U32, name="w_codes1", offset=codes1_at, align_bytes=ALIGN),
-        ]
-        w_scales = keep.tile([P, PASSES * M], U8, name="w_scales", align_bytes=ALIGN)
-        for g in range(PASSES):
-            nc.vector.quantize_mx(
-                out=w_codes[g][:].bitcast(FP8X4),
-                scales=w_scales[:, g * M : (g + 1) * M],
-                in_=w_bf[:, g * M * PACK : (g + 1) * M * PACK],
-            )
-
-        rate_sb = reused.tile([P, 1], F32, name="rate_sb", offset=rate_at, align_bytes=ALIGN)
+        rate_sb = keep.tile([P, 1], F32, name="rate_sb", tag="w_raw0", align_bytes=ALIGN)
         nc.sync.dma_start(rate_sb[:], rate)
-        gate_sb = [
-            keep.tile([P, S], F32, name=f"gate_sb{d}", tag=tag, align_bytes=ALIGN)
-            for d, tag in enumerate(("w_raw1", "w_bf"))
-        ]
+        coef = keep.tile([P, 2], F32, name="coef")
+        nc.gpsimd.tensor_scalar(coef[:, 0:1], rate_sb[:], -2.0, 0.0, ALU.mult, ALU.add)
+        nc.gpsimd.tensor_scalar(coef[:, 1:2], rate_sb[:], 0.5, 1.0, ALU.mult, ALU.add)
+        quantise(0)
+        picked = [keep.tile([P, S], U32, name=f"picked{g}", align_bytes=ALIGN) for g in range(PASSES)]
+        nc.vector.tensor_copy(picked[0][:], words[0][:].indirect(offs_sb[:]))
+        cast(1)
+        quantise(1)
+
+        gate_sb = [reused.tile([P, S], F32, name=f"gate_sb{d}", offset=d * S * 4, align_bytes=ALIGN) for d in range(2)]
         for d in range(2):
             nc.sync.dma_start(gate_sb[d][:], gate[d])
 
-        picked1 = reused.tile([P, S], U32, name="picked1", offset=picked1_at, align_bytes=ALIGN)
-        picked = (picked0, picked1)
+        def block(i):
+            return slice(i * P, (i + 1) * P)
+
         y = keep.tile([P, S], F32, name="y")
-        acc = [psum.tile([P, b - a], F32, name=f"acc{a}", tag=f"acc{a}") for a, b in STRETCHES]
+        acc = [psum.tile([P, P], F32, name=f"acc{c}", tag=f"acc{c}") for c in range(BLOCKS)]
 
         def product(c, g):
-            a, b = STRETCHES[c]
             nc.tensor.matmul_mx(
                 out=acc[c][:],
                 lhsT=w_codes[g][:].bitcast(FP8X4),
                 lhsT_scale=w_scales[:, g * M : (g + 1) * M],
-                rhs=picked[g][:, a:b].bitcast(FP8X4),
-                rhs_scale=picked_scales[:, g * S + a : g * S + b],
+                rhs=picked[g][:, block(c)].bitcast(FP8X4),
+                rhs_scale=picked_scales[:, g * S + c * P : g * S + (c + 1) * P],
                 start=(g == 0),
                 stop=(g == PASSES - 1),
             )
 
-        for c, (a, b) in enumerate(STRETCHES):
-            nc.vector.tensor_copy(picked1[:, a:b], words[1][:].indirect(offs_sb[:, a // LANE : b // LANE]))
+        for c in range(BLOCKS):
+            nc.vector.tensor_copy(picked[1][:, block(c)], words[1][:].indirect(offs_sb[:, c * P // LANE : (c + 1) * P // LANE]))
             product(c, 0)
             product(c, 1)
-            nc.scalar.activation(y[:, a:b], acc[c][:], ACT.Sigmoid)
+            nc.scalar.activation(y[:, block(c)], acc[c][:], ACT.Sigmoid)
 
-        coef = keep.tile([P, 2], F32, name="coef")
-        nc.scalar.activation(coef[:, 0:1], rate_sb[:], ACT.Copy, scale=-2.0)
-        nc.scalar.activation(coef[:, 1:2], rate_sb[:], ACT.Copy, scale=0.5, bias=1.0)
+        cut = EARLY * P
+        quad = keep.tile([P, cut], F32, name="quad")
+        react = keep.tile([P, cut], F32, name="react")
+        cubic = keep.tile([P, cut], F32, name="cubic")
+
+        def square(c):
+            nc.vector.tensor_tensor(quad[:, block(c)], y[:, block(c)], y[:, block(c)], ALU.mult)
+
+        def reaction(c):
+            cols = block(c)
+            nc.vector.scalar_tensor_tensor(cubic[:, cols], y[:, cols], 1.0, quad[:, cols], ALU.subtract, ALU.mult)
+            nc.scalar.activation(react[:, cols], cubic[:, cols], ACT.Copy, scale=coef[:, 0:1])
+
         sq = keep.tile([P, S], F32, name="sq", tag="sq")
-        factor = keep.tile([P, S], F32, name="factor")
-        for a, b in HALVES:
-            nc.scalar.activation(sq[:, a:b], y[:, a:b], ACT.Square, scale=-1.0, bias=half[:, 1:2])
-        for a, b in HALVES:
-            nc.scalar.activation(factor[:, a:b], sq[:, a:b], ACT.Identity, scale=coef[:, 0:1], bias=coef[:, 1:2])
+        factor = keep.tile([P, S - cut], F32, name="factor")
+        nc.scalar.activation(sq[:, cut:], y[:, cut:], ACT.Square, scale=-1.0, bias=half[:, 1:2])
+        nc.scalar.activation(factor[:], sq[:, cut:], ACT.Identity, scale=coef[:, 0:1], bias=coef[:, 1:2])
 
         def pull(dst, d, a, b):
             offsets = pos_sb[d][:, a // LANE : b // LANE]
@@ -159,42 +158,43 @@ def tile_picked_ygread_zeld_p_kernel(tc, x_words, x_scales, w1, gate, rate, offs
         def half_add(dst, pulled_part, other):
             nc.vector.scalar_tensor_tensor(dst, pulled_part, 0.5, other, ALU.mult, ALU.add)
 
-        def block(i):
-            return slice(i * P, (i + 1) * P)
-
         pulled0 = keep.tile([P, S], F32, name="pulled0")
-        own = keep.tile([P, S], F32, name="own")
-        turned = [psum.tile([P, P], F32, name=f"turned{i}") for i in range(CUT // P)]
-        turned_sb = keep.tile([P, CUT], F32, name="turned_sb")
-        back = [
-            psum.tile([P, b - a], F32, name=f"back{h}", tag=f"acc{STRETCHES[h][0]}")
-            for h, (a, b) in enumerate(TURNED_PIECES)
-        ]
-        part = keep.tile([P, S - CUT], F32, name="part")
+        own = keep.tile([P, S - cut], F32, name="own")
+        turned = [psum.tile([P, P], F32, name=f"turned{i}") for i in range(EARLY)]
+        turned_sb = keep.tile([P, cut], F32, name="turned_sb")
+        pieces = ((0, S // 2), (S // 2, cut))
+        back = [psum.tile([P, b - a], F32, name=f"back{h}", tag=f"acc{h}") for h, (a, b) in enumerate(pieces)]
+        part = keep.tile([P, S - cut], F32, name="part")
         res = keep.tile([P, S], F32, name="res")
 
-        for a, b in HALVES:
-            pull(pulled0, 0, a, b)
-        for i in range(CUT // P):
-            turn(turned[i][:], pulled0[:, block(i)], True, False)
-        for a, b in TURNED_PIECES:
-            nc.vector.tensor_tensor(own[:, a:b], y[:, a:b], factor[:, a:b], ALU.mult)
-            for i in range(a // P, b // P):
-                turn(turned[i][:], own[:, block(i)], False, True)
-        nc.vector.scalar_tensor_tensor(own[:, CUT:], factor[:, CUT:], 0.5, y[:, CUT:], ALU.mult, ALU.mult)
-        for h, (a, b) in enumerate(TURNED_PIECES):
+        for i in range(EARLY):
+            turn(turned[i][:], y[:, block(i)], True, False)
+        square(0)
+        for i in range(EARLY - 1):
+            square(i + 1)
+            reaction(i)
+            turn(turned[i][:], react[:, block(i)], False, False)
+        pull(pulled0, 0, *HALVES[0])
+        for i in range(EARLY - 1):
+            turn(turned[i][:], pulled0[:, block(i)], False, True)
+        reaction(EARLY - 1)
+        turn(turned[EARLY - 1][:], react[:, block(EARLY - 1)], False, False)
+        pull(pulled0, 0, *HALVES[1])
+        turn(turned[EARLY - 1][:], pulled0[:, block(EARLY - 1)], False, True)
+        nc.vector.scalar_tensor_tensor(own[:], factor[:], 0.5, y[:, cut:], ALU.mult, ALU.mult)
+        for h, (a, b) in enumerate(pieces):
             for i in range(a // P, b // P):
                 nc.scalar.activation(turned_sb[:, block(i)], turned[i][:], ACT.Copy, scale=0.5)
                 turn(back[h][:, block(i - a // P)], turned_sb[:, block(i)], True, True)
 
         pulled1 = keep.tile([P, S], F32, name="pulled1", tag="sq")
-        pull(pulled1, 1, CUT, S)
-        half_add(part[:], pulled0[:, CUT:], own[:, CUT:])
-        pull(pulled1, 1, *TURNED_PIECES[0])
-        half_add(res[:, CUT:], pulled1[:, CUT:], part[:])
-        nc.sync.dma_start(out[:, CUT:], res[:, CUT:])
-        pull(pulled1, 1, *TURNED_PIECES[1])
+        pull(pulled1, 1, cut, S)
+        half_add(part[:], pulled0[:, cut:], own[:])
+        pull(pulled1, 1, *pieces[0])
+        half_add(res[:, cut:], pulled1[:, cut:], part[:])
+        nc.sync.dma_start(out[:, cut:], res[:, cut:])
+        pull(pulled1, 1, *pieces[1])
         for h, queue in enumerate((nc.sync, nc.scalar)):
-            a, b = TURNED_PIECES[h]
+            a, b = pieces[h]
             half_add(res[:, a:b], pulled1[:, a:b], back[h][:])
             queue.dma_start(out[:, a:b], res[:, a:b])

@@ -94,9 +94,9 @@ def tile_picked_ygread_zeld_p_kernel(tc, x_words, x_scales, w1, gate, rate, offs
             )
         rate_sb = keep.tile([P, 1], F32, name="rate_sb", tag="w_raw0", align_bytes=ALIGN)
         nc.sync.dma_start(rate_sb[:], rate)
-        coef = keep.tile([P, 2], F32, name="coef")
-        nc.gpsimd.tensor_scalar(coef[:, 0:1], rate_sb[:], -2.0, 0.0, ALU.mult, ALU.add)
-        nc.gpsimd.tensor_scalar(coef[:, 1:2], rate_sb[:], 0.5, 1.0, ALU.mult, ALU.add)
+        coef = keep.tile([P, 3], F32, name="coef")
+        for j, (slope, base) in enumerate(((-2.0, 0.0), (-1.0, 0.0), (0.25, 0.5))):
+            nc.gpsimd.tensor_scalar(coef[:, j : j + 1], rate_sb[:], slope, base, ALU.mult, ALU.add)
         quantise(0)
         picked = [keep.tile([P, S], U32, name=f"picked{g}", align_bytes=ALIGN) for g in range(PASSES)]
         nc.vector.tensor_copy(picked[0][:], words[0][:].indirect(offs_sb[:]))
@@ -130,23 +130,11 @@ def tile_picked_ygread_zeld_p_kernel(tc, x_words, x_scales, w1, gate, rate, offs
             product(c, 1)
             nc.scalar.activation(y[:, block(c)], acc[c][:], ACT.Sigmoid)
 
-        cut = EARLY * P
-        quad = keep.tile([P, cut], F32, name="quad")
-        react = keep.tile([P, cut], F32, name="react")
-        cubic = keep.tile([P, cut], F32, name="cubic")
-
-        def square(c):
-            nc.vector.tensor_tensor(quad[:, block(c)], y[:, block(c)], y[:, block(c)], ALU.mult)
-
-        def reaction(c):
-            cols = block(c)
-            nc.vector.scalar_tensor_tensor(cubic[:, cols], y[:, cols], 1.0, quad[:, cols], ALU.subtract, ALU.mult)
-            nc.scalar.activation(react[:, cols], cubic[:, cols], ACT.Copy, scale=coef[:, 0:1])
-
-        sq = keep.tile([P, S], F32, name="sq", tag="sq")
-        factor = keep.tile([P, S - cut], F32, name="factor")
-        nc.scalar.activation(sq[:, cut:], y[:, cut:], ACT.Square, scale=-1.0, bias=half[:, 1:2])
-        nc.scalar.activation(factor[:], sq[:, cut:], ACT.Identity, scale=coef[:, 0:1], bias=coef[:, 1:2])
+        last = EARLY * P
+        mid = S // 2
+        quad = keep.tile([P, last], F32, name="quad")
+        cubic = keep.tile([P, last], F32, name="cubic")
+        react = keep.tile([P, last], F32, name="react")
 
         def pull(dst, d, a, b):
             offsets = pos_sb[d][:, a // LANE : b // LANE]
@@ -158,14 +146,29 @@ def tile_picked_ygread_zeld_p_kernel(tc, x_words, x_scales, w1, gate, rate, offs
         def half_add(dst, pulled_part, other):
             nc.vector.scalar_tensor_tensor(dst, pulled_part, 0.5, other, ALU.mult, ALU.add)
 
+        sq = keep.tile([P, S], F32, name="sq", tag="sq")
+        factor = keep.tile([P, P], F32, name="factor")
+        own = keep.tile([P, P], F32, name="own")
         pulled0 = keep.tile([P, S], F32, name="pulled0")
-        own = keep.tile([P, S - cut], F32, name="own")
         turned = [psum.tile([P, P], F32, name=f"turned{i}") for i in range(EARLY)]
-        turned_sb = keep.tile([P, cut], F32, name="turned_sb")
-        pieces = ((0, S // 2), (S // 2, cut))
+        turned_sb = keep.tile([P, last], F32, name="turned_sb")
+        pieces = ((0, mid), (mid, last))
         back = [psum.tile([P, b - a], F32, name=f"back{h}", tag=f"acc{h}") for h, (a, b) in enumerate(pieces)]
-        part = keep.tile([P, S - cut], F32, name="part")
+        part = keep.tile([P, P], F32, name="part")
         res = keep.tile([P, S], F32, name="res")
+
+        nc.scalar.activation(sq[:, last:], y[:, last:], ACT.Square, scale=-1.0, bias=half[:, 1:2])
+        nc.scalar.activation(factor[:], sq[:, last:], ACT.Identity, scale=coef[:, 1:2], bias=coef[:, 2:3])
+
+        def square(i):
+            cols = block(i)
+            nc.vector.scalar_tensor_tensor(quad[:, cols], y[:, cols], 1.0, y[:, cols], ALU.subtract, ALU.mult)
+
+        def reaction(i):
+            cols = block(i)
+            nc.vector.tensor_tensor(cubic[:, cols], quad[:, cols], y[:, cols], ALU.mult)
+            nc.scalar.activation(react[:, cols], cubic[:, cols], ACT.Copy, scale=coef[:, 0:1])
+            turn(turned[i][:], react[:, cols], False, False)
 
         for i in range(EARLY):
             turn(turned[i][:], y[:, block(i)], True, False)
@@ -173,28 +176,25 @@ def tile_picked_ygread_zeld_p_kernel(tc, x_words, x_scales, w1, gate, rate, offs
         for i in range(EARLY - 1):
             square(i + 1)
             reaction(i)
-            turn(turned[i][:], react[:, block(i)], False, False)
-        pull(pulled0, 0, *HALVES[0])
+        pull(pulled0, 0, 0, mid)
         for i in range(EARLY - 1):
             turn(turned[i][:], pulled0[:, block(i)], False, True)
         reaction(EARLY - 1)
-        turn(turned[EARLY - 1][:], react[:, block(EARLY - 1)], False, False)
-        pull(pulled0, 0, *HALVES[1])
+        pull(pulled0, 0, mid, S)
         turn(turned[EARLY - 1][:], pulled0[:, block(EARLY - 1)], False, True)
-        nc.vector.scalar_tensor_tensor(own[:], factor[:], 0.5, y[:, cut:], ALU.mult, ALU.mult)
+        nc.vector.tensor_tensor(own[:], y[:, last:], factor[:], ALU.mult)
         for h, (a, b) in enumerate(pieces):
             for i in range(a // P, b // P):
                 nc.scalar.activation(turned_sb[:, block(i)], turned[i][:], ACT.Copy, scale=0.5)
                 turn(back[h][:, block(i - a // P)], turned_sb[:, block(i)], True, True)
 
         pulled1 = keep.tile([P, S], F32, name="pulled1", tag="sq")
-        pull(pulled1, 1, cut, S)
-        half_add(part[:], pulled0[:, cut:], own[:])
-        pull(pulled1, 1, *pieces[0])
-        half_add(res[:, cut:], pulled1[:, cut:], part[:])
-        nc.sync.dma_start(out[:, cut:], res[:, cut:])
-        pull(pulled1, 1, *pieces[1])
-        for h, queue in enumerate((nc.sync, nc.scalar)):
-            a, b = pieces[h]
-            half_add(res[:, a:b], pulled1[:, a:b], back[h][:])
-            queue.dma_start(out[:, a:b], res[:, a:b])
+        pull(pulled1, 1, 0, mid)
+        half_add(part[:], pulled0[:, last:], own[:])
+        pull(pulled1, 1, mid, S)
+        half_add(res[:, :mid], pulled1[:, :mid], back[0][:])
+        nc.sync.dma_start(out[:, :mid], res[:, :mid])
+        half_add(res[:, last:], pulled1[:, last:], part[:])
+        nc.scalar.dma_start(out[:, last:], res[:, last:])
+        half_add(res[:, mid:last], pulled1[:, mid:last], back[1][:])
+        nc.sync.dma_start(out[:, mid:last], res[:, mid:last])

@@ -195,6 +195,6 @@ def tile_picked_ygread_zeld_p_kernel(tc, x_words, x_scales, w1, gate, rate, offs
         half_add(res[:, :mid], pulled1[:, :mid], back[0][:])
         nc.sync.dma_start(out[:, :mid], res[:, :mid])
         half_add(res[:, last:], pulled1[:, last:], part[:])
-        nc.scalar.dma_start(out[:, last:], res[:, last:])
+        nc.sync.dma_start(out[:, last:], res[:, last:])
         half_add(res[:, mid:last], pulled1[:, mid:last], back[1][:])
-        nc.sync.dma_start(out[:, mid:last], res[:, mid:last])
+        nc.scalar.dma_start(out[:, mid:last], res[:, mid:last])

@@ -49,7 +49,6 @@ def tile_picked_ygread_zeld_p_kernel(tc, x_words, x_scales, w1, gate, rate, offs
 
         half = keep.tile([P, 2], F32, name="half")
         nc.vector.memset(half[:, 0:1], 0.0)
-        nc.scalar.activation(half[:, 1:2], half[:, 0:1], ACT.Sigmoid)
 
         ident = keep.tile([P, P], F32, name="ident")
         make_identity(nc, ident[:])
@@ -59,8 +58,9 @@ def tile_picked_ygread_zeld_p_kernel(tc, x_words, x_scales, w1, gate, rate, offs
         nc.vector.memset(picked_scales[:].bitcast(I32), 0)
 
         nc.sync.dma_start(offs_sb[:], offs)
-        for g, queue in enumerate((nc.scalar, nc.sync)):
-            queue.dma_start(scale_rows[g:QUAD:PASSES, :].bitcast(I32), x_scales[g].bitcast(I32))
+        for g in range(PASSES):
+            nc.scalar.dma_start(scale_rows[g:QUAD:PASSES, :].bitcast(I32), x_scales[g].bitcast(I32))
+        nc.scalar.activation(half[:, 1:2], half[:, 0:1], ACT.Sigmoid)
         for g in range(PASSES):
             k_rows = w1[P * PACK * g : P * PACK * (g + 1), :]
             nc.sync.dma_start(w_raw[g][:], k_rows.rearrange("(p t) m -> p t m", t=PACK))

@@ -133,23 +133,13 @@ def tile_picked_ygread_zeld_p_kernel(tc, x_words, x_scales, w1, gate, rate, offs
         last = EARLY * P
         mid = S // 2
         quad = keep.tile([P, last], F32, name="quad")
-        cubic = keep.tile([P, last], F32, name="cubic")
         react = keep.tile([P, last], F32, name="react")
-
-        def pull(dst, d, a, b):
-            offsets = pos_sb[d][:, a // LANE : b // LANE]
-            nc.vector.tensor_tensor(dst[:, a:b], y[:].indirect(offsets), gate_sb[d][:, a:b], ALU.mult)
-
-        def turn(dst, src, start, stop):
-            nc.tensor.matmul(dst, src, ident[:], start=start, stop=stop, is_transpose=True)
-
-        def half_add(dst, pulled_part, other):
-            nc.vector.scalar_tensor_tensor(dst, pulled_part, 0.5, other, ALU.mult, ALU.add)
-
-        sq = keep.tile([P, S], F32, name="sq", tag="sq")
+        sq = keep.tile([P, P], F32, name="sq")
         factor = keep.tile([P, P], F32, name="factor")
         own = keep.tile([P, P], F32, name="own")
-        pulled0 = keep.tile([P, S], F32, name="pulled0")
+        first = keep.tile([P, S], F32, name="first")
+        fetched = keep.tile([P, last], F32, name="fetched")
+        second = keep.tile([P, S], F32, name="second")
         turned = [psum.tile([P, P], F32, name=f"turned{i}") for i in range(EARLY)]
         turned_sb = keep.tile([P, last], F32, name="turned_sb")
         pieces = ((0, mid), (mid, last))
@@ -157,8 +147,17 @@ def tile_picked_ygread_zeld_p_kernel(tc, x_words, x_scales, w1, gate, rate, offs
         part = keep.tile([P, P], F32, name="part")
         res = keep.tile([P, S], F32, name="res")
 
-        nc.scalar.activation(sq[:, last:], y[:, last:], ACT.Square, scale=-1.0, bias=half[:, 1:2])
-        nc.scalar.activation(factor[:], sq[:, last:], ACT.Identity, scale=coef[:, 1:2], bias=coef[:, 2:3])
+        def window(d, a, b):
+            return y[:].indirect(pos_sb[d][:, a // LANE : b // LANE])
+
+        def pull(dst, d, a, b):
+            nc.vector.tensor_tensor(dst[:, a:b], window(d, a, b), gate_sb[d][:, a:b], ALU.mult)
+
+        def turn(dst, src, start, stop):
+            nc.tensor.matmul(dst, src, ident[:], start=start, stop=stop, is_transpose=True)
+
+        def half_add(dst, pulled_part, other):
+            nc.vector.scalar_tensor_tensor(dst, pulled_part, 0.5, other, ALU.mult, ALU.add)
 
         def square(i):
             cols = block(i)
@@ -166,9 +165,13 @@ def tile_picked_ygread_zeld_p_kernel(tc, x_words, x_scales, w1, gate, rate, offs
 
         def reaction(i):
             cols = block(i)
-            nc.vector.tensor_tensor(cubic[:, cols], quad[:, cols], y[:, cols], ALU.mult)
-            nc.scalar.activation(react[:, cols], cubic[:, cols], ACT.Copy, scale=coef[:, 0:1])
+            nc.vector.scalar_tensor_tensor(react[:, cols], quad[:, cols], coef[:, 0:1], y[:, cols], ALU.mult, ALU.mult)
             turn(turned[i][:], react[:, cols], False, False)
+
+        nc.scalar.activation(sq[:], y[:, last:], ACT.Square, scale=-1.0, bias=half[:, 1:2])
+        nc.scalar.activation(fetched[:, :mid], window(1, 0, mid), ACT.Copy)
+        nc.scalar.activation(factor[:], sq[:], ACT.Identity, scale=coef[:, 1:2], bias=coef[:, 2:3])
+        nc.scalar.activation(fetched[:, mid:], window(1, mid, last), ACT.Copy)
 
         for i in range(EARLY):
             turn(turned[i][:], y[:, block(i)], True, False)
@@ -176,25 +179,25 @@ def tile_picked_ygread_zeld_p_kernel(tc, x_words, x_scales, w1, gate, rate, offs
         for i in range(EARLY - 1):
             square(i + 1)
             reaction(i)
-        pull(pulled0, 0, 0, mid)
+        pull(first, 0, 0, mid)
         for i in range(EARLY - 1):
-            turn(turned[i][:], pulled0[:, block(i)], False, True)
+            turn(turned[i][:], first[:, block(i)], False, True)
         reaction(EARLY - 1)
-        pull(pulled0, 0, mid, S)
-        turn(turned[EARLY - 1][:], pulled0[:, block(EARLY - 1)], False, True)
-        nc.vector.tensor_tensor(own[:], y[:, last:], factor[:], ALU.mult)
+        pull(first, 0, mid, last)
+        turn(turned[EARLY - 1][:], first[:, block(EARLY - 1)], False, True)
+        pull(first, 0, last, S)
         for h, (a, b) in enumerate(pieces):
             for i in range(a // P, b // P):
                 nc.scalar.activation(turned_sb[:, block(i)], turned[i][:], ACT.Copy, scale=0.5)
                 turn(back[h][:, block(i - a // P)], turned_sb[:, block(i)], True, True)
 
-        pulled1 = keep.tile([P, S], F32, name="pulled1", tag="sq")
-        pull(pulled1, 1, 0, mid)
-        half_add(part[:], pulled0[:, last:], own[:])
-        pull(pulled1, 1, mid, S)
-        half_add(res[:, :mid], pulled1[:, :mid], back[0][:])
-        nc.sync.dma_start(out[:, :mid], res[:, :mid])
-        half_add(res[:, last:], pulled1[:, last:], part[:])
+        nc.vector.tensor_tensor(own[:], y[:, last:], factor[:], ALU.mult)
+        pull(second, 1, last, S)
+        half_add(part[:], first[:, last:], own[:])
+        nc.vector.tensor_tensor(second[:, :last], fetched[:], gate_sb[1][:, :last], ALU.mult)
+        half_add(res[:, last:], second[:, last:], part[:])
         nc.sync.dma_start(out[:, last:], res[:, last:])
-        half_add(res[:, mid:last], pulled1[:, mid:last], back[1][:])
+        half_add(res[:, :mid], second[:, :mid], back[0][:])
+        nc.sync.dma_start(out[:, :mid], res[:, :mid])
+        half_add(res[:, mid:last], second[:, mid:last], back[1][:])
         nc.scalar.dma_start(out[:, mid:last], res[:, mid:last])

@@ -134,12 +134,12 @@ def tile_picked_ygread_zeld_p_kernel(tc, x_words, x_scales, w1, gate, rate, offs
         mid = S // 2
         quad = keep.tile([P, last], F32, name="quad")
         react = keep.tile([P, last], F32, name="react")
-        sq = keep.tile([P, P], F32, name="sq")
+        sq = keep.tile([P, P], F32, name="sq", tag="sq")
         factor = keep.tile([P, P], F32, name="factor")
         own = keep.tile([P, P], F32, name="own")
         first = keep.tile([P, S], F32, name="first")
         fetched = keep.tile([P, last], F32, name="fetched")
-        second = keep.tile([P, S], F32, name="second")
+        second = keep.tile([P, last], F32, name="second")
         turned = [psum.tile([P, P], F32, name=f"turned{i}") for i in range(EARLY)]
         turned_sb = keep.tile([P, last], F32, name="turned_sb")
         pieces = ((0, mid), (mid, last))
@@ -151,7 +151,7 @@ def tile_picked_ygread_zeld_p_kernel(tc, x_words, x_scales, w1, gate, rate, offs
             return y[:].indirect(pos_sb[d][:, a // LANE : b // LANE])
 
         def pull(dst, d, a, b):
-            nc.vector.tensor_tensor(dst[:, a:b], window(d, a, b), gate_sb[d][:, a:b], ALU.mult)
+            nc.vector.tensor_tensor(dst, window(d, a, b), gate_sb[d][:, a:b], ALU.mult)
 
         def turn(dst, src, start, stop):
             nc.tensor.matmul(dst, src, ident[:], start=start, stop=stop, is_transpose=True)
@@ -179,25 +179,27 @@ def tile_picked_ygread_zeld_p_kernel(tc, x_words, x_scales, w1, gate, rate, offs
         for i in range(EARLY - 1):
             square(i + 1)
             reaction(i)
-        pull(first, 0, 0, mid)
+        pull(first[:, :mid], 0, 0, mid)
         for i in range(EARLY - 1):
             turn(turned[i][:], first[:, block(i)], False, True)
         reaction(EARLY - 1)
-        pull(first, 0, mid, last)
+        pull(first[:, mid:last], 0, mid, last)
         turn(turned[EARLY - 1][:], first[:, block(EARLY - 1)], False, True)
-        pull(first, 0, last, S)
+        pull(first[:, last:], 0, last, S)
         for h, (a, b) in enumerate(pieces):
             for i in range(a // P, b // P):
                 nc.scalar.activation(turned_sb[:, block(i)], turned[i][:], ACT.Copy, scale=0.5)
                 turn(back[h][:, block(i - a // P)], turned_sb[:, block(i)], True, True)
 
         nc.vector.tensor_tensor(own[:], y[:, last:], factor[:], ALU.mult)
-        pull(second, 1, last, S)
+        second_last = keep.tile([P, P], F32, name="second_last", tag="sq")
+        pull(second_last[:], 1, last, S)
+        nc.vector.tensor_tensor(second[:, :mid], fetched[:, :mid], gate_sb[1][:, :mid], ALU.mult)
         half_add(part[:], first[:, last:], own[:])
-        nc.vector.tensor_tensor(second[:, :last], fetched[:], gate_sb[1][:, :last], ALU.mult)
-        half_add(res[:, last:], second[:, last:], part[:])
-        nc.sync.dma_start(out[:, last:], res[:, last:])
+        nc.vector.tensor_tensor(second[:, mid:], fetched[:, mid:], gate_sb[1][:, mid:last], ALU.mult)
         half_add(res[:, :mid], second[:, :mid], back[0][:])
         nc.sync.dma_start(out[:, :mid], res[:, :mid])
+        half_add(res[:, last:], second_last[:], part[:])
+        nc.scalar.dma_start(out[:, last:], res[:, last:])
         half_add(res[:, mid:last], second[:, mid:last], back[1][:])
         nc.scalar.dma_start(out[:, mid:last], res[:, mid:last])

@@ -200,6 +200,6 @@ def tile_picked_ygread_zeld_p_kernel(tc, x_words, x_scales, w1, gate, rate, offs
         half_add(res[:, :mid], second[:, :mid], back[0][:])
         nc.sync.dma_start(out[:, :mid], res[:, :mid])
         half_add(res[:, last:], second_last[:], part[:])
-        nc.scalar.dma_start(out[:, last:], res[:, last:])
+        nc.sync.dma_start(out[:, last:], res[:, last:])
         half_add(res[:, mid:last], second[:, mid:last], back[1][:])
         nc.scalar.dma_start(out[:, mid:last], res[:, mid:last])

@@ -57,13 +57,14 @@ def tile_picked_ygread_zeld_p_kernel(tc, x_words, x_scales, w1, gate, rate, offs
         nc.vector.memset(scale_rows[2 * QUAD : P, :].bitcast(I32), 0)
         nc.vector.memset(picked_scales[:].bitcast(I32), 0)
 
-        nc.sync.dma_start(offs_sb[:], offs)
         for g in range(PASSES):
             nc.scalar.dma_start(scale_rows[g:QUAD:PASSES, :].bitcast(I32), x_scales[g].bitcast(I32))
         nc.scalar.activation(half[:, 1:2], half[:, 0:1], ACT.Sigmoid)
         for g in range(PASSES):
             k_rows = w1[P * PACK * g : P * PACK * (g + 1), :]
             nc.sync.dma_start(w_raw[g][:], k_rows.rearrange("(p t) m -> p t m", t=PACK))
+            if g == 0:
+                nc.sync.dma_start(offs_sb[:], offs)
             nc.sync.dma_start(words[g][:].bitcast(I32), x_words[g].rearrange("p c r -> p (c r)").bitcast(I32))
         nc.sync.dma_start(pos_sb[0][:], pos1)
         nc.sync.dma_start(pos_sb[1][:], pos2)

from contextlib import ExitStack

import concourse.mybir as mybir
from concourse.masks import make_identity

K, T, S, M = 1024, 1024, 512, 128
FLOPS = 2 * K * M * S

F32 = mybir.dt.float32
BF16 = mybir.dt.bfloat16
I32 = mybir.dt.int32
U32 = mybir.dt.uint32
U16 = mybir.dt.uint16
U8 = mybir.dt.uint8
FP8X4 = mybir.dt.float8_e4m3fn_x4
ACT = mybir.ActivationFunctionType
ALU = mybir.AluOpType

P = 128
QUAD = 32
PACK = 4
PASSES = K // (P * PACK)
ROWS = 4
LANE = 16
ALIGN = 64
BLOCKS = S // P
EARLY = 3
HALVES = ((0, S // 2), (S // 2, S))


def tile_picked_ygread_zeld_p_kernel(tc, x_words, x_scales, w1, gate, rate, offs, pos1, pos2, out):
    nc = tc.nc
    with ExitStack() as ctx:
        keep = ctx.enter_context(tc.tile_pool(name="keep", bufs=1))
        reused = ctx.enter_context(tc.tile_pool(name="reused", bufs=1))
        psum = ctx.enter_context(tc.psum_pool(name="psum", bufs=1))

        offs_sb = keep.tile([P, S // LANE], U16, name="offs_sb")
        pos_sb = [keep.tile([P, S // LANE], U16, name=f"pos_sb{d}") for d in range(2)]
        words = [
            reused.tile([P, T], U32, name="words0", offset=0, align_bytes=ALIGN),
            keep.tile([P, T], U32, name="words1", align_bytes=ALIGN),
        ]
        scale_rows = keep.tile([P, T], U8, name="scale_rows", align_bytes=ALIGN)
        w_raw = [keep.tile([P, PACK, M], F32, name=f"w_raw{g}", tag=f"w_raw{g}", align_bytes=ALIGN) for g in range(PASSES)]
        picked_rows = keep.tile([P, S], U8, name="picked_rows")
        picked_scales = keep.tile([P, PASSES * S], U8, name="picked_scales", align_bytes=ALIGN)


        half = keep.tile([P, 2], F32, name="half")
        nc.vector.memset(half[:, 0:1], 0.0)

        ident = keep.tile([P, P], F32, name="ident")
        make_identity(nc, ident[:])

        nc.vector.memset(scale_rows[QUAD : 2 * QUAD, :].bitcast(I32), 0)
        nc.vector.memset(scale_rows[2 * QUAD : P, :].bitcast(I32), 0)
        nc.vector.memset(picked_scales[:].bitcast(I32), 0)

        for g in range(PASSES):
            nc.scalar.dma_start(scale_rows[g:QUAD:PASSES, :].bitcast(I32), x_scales[g].bitcast(I32))
        nc.scalar.activation(half[:, 1:2], half[:, 0:1], ACT.Sigmoid)
        for g in range(PASSES):
            k_rows = w1[P * PACK * g : P * PACK * (g + 1), :]
            nc.sync.dma_start(w_raw[g][:], k_rows.rearrange("(p t) m -> p t m", t=PACK))
            if g == 0:
                nc.sync.dma_start(offs_sb[:], offs)
            nc.sync.dma_start(words[g][:].bitcast(I32), x_words[g].rearrange("p c r -> p (c r)").bitcast(I32))
        nc.sync.dma_start(pos_sb[0][:], pos1)
        nc.sync.dma_start(pos_sb[1][:], pos2)


        nc.vector.tensor_copy(picked_rows[:], scale_rows[:].indirect(offs_sb[:]))

        w_bf = [keep.tile([P, M * PACK], BF16, name=f"w_bf{g}", align_bytes=ALIGN) for g in range(PASSES)]
        w_codes = [keep.tile([P, M], U32, name=f"w_codes{g}", align_bytes=ALIGN) for g in range(PASSES)]
        w_scales = keep.tile([P, PASSES * M], U8, name="w_scales", align_bytes=ALIGN)

        def cast(g):
            nc.scalar.copy(
                w_bf[g][:].rearrange("p (c i t) -> p c t i", i=PACK, t=PACK),
                w_raw[g][:].rearrange("p t (c i) -> p c t i", i=PACK),
            )

        def quantise(g):
            nc.vector.quantize_mx(
                out=w_codes[g][:].bitcast(FP8X4), scales=w_scales[:, g * M : (g + 1) * M], in_=w_bf[g][:]
            )

        cast(0)
        for q in range(P // QUAD):
            nc.sync.dma_start(
                picked_scales[QUAD * q : QUAD * q + ROWS, :].bitcast(I32),
                picked_rows[PASSES * ROWS * q : PASSES * ROWS * (q + 1), :].bitcast(I32),
            )
        rate_sb = keep.tile([P, 1], F32, name="rate_sb", tag="w_raw0", align_bytes=ALIGN)
        nc.sync.dma_start(rate_sb[:], rate)
        coef = keep.tile([P, 3], F32, name="coef")
        for j, (slope, base) in enumerate(((-2.0, 0.0), (-1.0, 0.0), (0.25, 0.5))):
            nc.gpsimd.tensor_scalar(coef[:, j : j + 1], rate_sb[:], slope, base, ALU.mult, ALU.add)
        quantise(0)
        picked = [keep.tile([P, S], U32, name=f"picked{g}", align_bytes=ALIGN) for g in range(PASSES)]
        nc.vector.tensor_copy(picked[0][:], words[0][:].indirect(offs_sb[:]))
        cast(1)
        quantise(1)

        gate_sb = [reused.tile([P, S], F32, name=f"gate_sb{d}", offset=d * S * 4, align_bytes=ALIGN) for d in range(2)]
        for d in range(2):
            nc.sync.dma_start(gate_sb[d][:], gate[d])

        def block(i):
            return slice(i * P, (i + 1) * P)

        y = keep.tile([P, S], F32, name="y")
        acc = [psum.tile([P, P], F32, name=f"acc{c}", tag=f"acc{c}") for c in range(BLOCKS)]

        def product(c, g):
            nc.tensor.matmul_mx(
                out=acc[c][:],
                lhsT=w_codes[g][:].bitcast(FP8X4),
                lhsT_scale=w_scales[:, g * M : (g + 1) * M],
                rhs=picked[g][:, block(c)].bitcast(FP8X4),
                rhs_scale=picked_scales[:, g * S + c * P : g * S + (c + 1) * P],
                start=(g == 0),
                stop=(g == PASSES - 1),
            )

        for c in range(BLOCKS):
            nc.vector.tensor_copy(picked[1][:, block(c)], words[1][:].indirect(offs_sb[:, c * P // LANE : (c + 1) * P // LANE]))
            product(c, 0)
            product(c, 1)
            nc.scalar.activation(y[:, block(c)], acc[c][:], ACT.Sigmoid)

        last = EARLY * P
        mid = S // 2
        quad = keep.tile([P, last], F32, name="quad")
        react = keep.tile([P, last], F32, name="react")
        sq = keep.tile([P, P], F32, name="sq", tag="sq")
        factor = keep.tile([P, P], F32, name="factor")
        own = keep.tile([P, P], F32, name="own")
        first = keep.tile([P, S], F32, name="first")
        fetched = keep.tile([P, last], F32, name="fetched")
        second = keep.tile([P, last], F32, name="second")
        turned = [psum.tile([P, P], F32, name=f"turned{i}") for i in range(EARLY)]
        turned_sb = keep.tile([P, last], F32, name="turned_sb")
        pieces = ((0, mid), (mid, last))
        back = [psum.tile([P, b - a], F32, name=f"back{h}", tag=f"acc{h}") for h, (a, b) in enumerate(pieces)]
        part = keep.tile([P, P], F32, name="part")
        res = keep.tile([P, S], F32, name="res")

        def window(d, a, b):
            return y[:].indirect(pos_sb[d][:, a // LANE : b // LANE])

        def pull(dst, d, a, b):
            nc.vector.tensor_tensor(dst, window(d, a, b), gate_sb[d][:, a:b], ALU.mult)

        def turn(dst, src, start, stop):
            nc.tensor.matmul(dst, src, ident[:], start=start, stop=stop, is_transpose=True)

        def half_add(dst, pulled_part, other):
            nc.vector.scalar_tensor_tensor(dst, pulled_part, 0.5, other, ALU.mult, ALU.add)

        def square(i):
            cols = block(i)
            nc.vector.scalar_tensor_tensor(quad[:, cols], y[:, cols], 1.0, y[:, cols], ALU.subtract, ALU.mult)

        def reaction(i):
            cols = block(i)
            nc.vector.scalar_tensor_tensor(react[:, cols], quad[:, cols], coef[:, 0:1], y[:, cols], ALU.mult, ALU.mult)
            turn(turned[i][:], react[:, cols], False, False)

        nc.scalar.activation(sq[:], y[:, last:], ACT.Square, scale=-1.0, bias=half[:, 1:2])
        nc.scalar.activation(fetched[:, :mid], window(1, 0, mid), ACT.Copy)
        nc.scalar.activation(factor[:], sq[:], ACT.Identity, scale=coef[:, 1:2], bias=coef[:, 2:3])
        nc.scalar.activation(fetched[:, mid:], window(1, mid, last), ACT.Copy)

        for i in range(EARLY):
            turn(turned[i][:], y[:, block(i)], True, False)
        square(0)
        for i in range(EARLY - 1):
            square(i + 1)
            reaction(i)
        pull(first[:, :mid], 0, 0, mid)
        for i in range(EARLY - 1):
            turn(turned[i][:], first[:, block(i)], False, True)
        reaction(EARLY - 1)
        pull(first[:, mid:last], 0, mid, last)
        turn(turned[EARLY - 1][:], first[:, block(EARLY - 1)], False, True)
        pull(first[:, last:], 0, last, S)
        for h, (a, b) in enumerate(pieces):
            for i in range(a // P, b // P):
                nc.scalar.activation(turned_sb[:, block(i)], turned[i][:], ACT.Copy, scale=0.5)
                turn(back[h][:, block(i - a // P)], turned_sb[:, block(i)], True, True)

        nc.vector.tensor_tensor(own[:], y[:, last:], factor[:], ALU.mult)
        second_last = keep.tile([P, P], F32, name="second_last", tag="sq")
        pull(second_last[:], 1, last, S)
        nc.vector.tensor_tensor(second[:, :mid], fetched[:, :mid], gate_sb[1][:, :mid], ALU.mult)
        half_add(part[:], first[:, last:], own[:])
        nc.vector.tensor_tensor(second[:, mid:], fetched[:, mid:], gate_sb[1][:, mid:last], ALU.mult)
        half_add(res[:, :mid], second[:, :mid], back[0][:])
        nc.sync.dma_start(out[:, :mid], res[:, :mid])
        half_add(res[:, last:], second_last[:], part[:])
        nc.sync.dma_start(out[:, last:], res[:, last:])
        half_add(res[:, mid:last], second[:, mid:last], back[1][:])
        nc.scalar.dma_start(out[:, mid:last], res[:, mid:last])
